import numpy as np, ml_dtypes
CORES = [3,7,11,15,131,135,139,143]
N = 8
import mx_ref
BF = ml_dtypes.bfloat16
def pick(q, e):
    c = np.concatenate([q[0].reshape(128, -1, 4), np.zeros((128, 1, 4), np.uint8)], axis=1); s = np.concatenate([q[1], np.ones((16, 1), np.uint8)], axis=1)
    return (np.ascontiguousarray(c[:, e].reshape(128, -1)), np.ascontiguousarray(s[:, e]))
def join(*qs):
    return (np.concatenate([q[0] for q in qs], axis=1), np.concatenate([q[1] for q in qs], axis=1))
def put(q, e, v):
    c, s = q[0].reshape(128, -1, 4).copy(), q[1].copy(); c[:, e] = v[0].reshape(128, -1, 4); s[:, e] = v[1]
    return (c.reshape(128, -1), s)
def pk(c, s):
    return (np.ascontiguousarray(c), mx_ref.live(s))
def emit(q):
    return q[0], q[1]
def cut(t, i, w=512):
    return t[:, w * i:w * i + w]
def f(rng, *shape):
    return mx_ref.flush((rng.standard_normal(shape, dtype=np.float32) * np.exp2(rng.integers(-2, 3, shape[:-1] + (1,)))).astype(BF))
def wide(rng, *shape, cols=0):
    v = rng.standard_normal(shape, dtype=np.float32) * np.exp2(rng.integers(-12, 13, shape)).astype(np.float32)
    if cols: v *= np.repeat(np.exp2(rng.integers(-cols, cols + 1, shape[:-2] + (1, shape[-1] // 4))) * (rng.random(shape[:-2] + (1, shape[-1] // 4)) > 0.0625), 4, axis=-1).astype(np.float32)
    return mx_ref.flush(v.astype(BF))
P, R, O = 512, 4, 1
C = P // 16
CLOUD = np.arange(N * P) % P // C
def same(t):
    return np.stack([t] * N)
def sizes(rng, *shape):
    return (1 + rng.random(shape, dtype=np.float32)) * (1 - 2 * rng.integers(0, 2, shape)).astype(np.float32)
def setup_inputs(rng):
    return {"x": f(rng, N, 128, 4 * P), "seed": same(f(rng, 128, 64)), "w": f(rng, N, 128, 512 * O)}
def setup_inputs_again(rng):
    d = setup_inputs(rng)
    half = rng.permutation(16) < 8
    four = rng.permutation(np.flatnonzero(half))[:4]
    huge, minus = np.isin(np.arange(16), four), np.isin(np.arange(16), four[:2])
    x, s = sizes(rng, N, 128, 4 * P), sizes(rng, 128, 64)
    x = np.where(np.repeat(half, 4 * C), np.abs(x), x)
    s = np.where(np.repeat(half, 4), np.abs(s), s)
    for b in np.flatnonzero(half):
        r, j = int(rng.integers(0, N)), int(b * C + rng.integers(0, C))
        if minus[b]: r, j = 0, int(b * C)
        x[r, :, 4 * j:4 * j + 4] *= np.float32(0.5 if huge[b] else 2.0 ** -8)
    by = np.where(huge, np.float32(2.0 ** 29), np.float32(1))
    x, s = x * np.repeat(by, 4 * C), s * np.repeat(np.where(minus, -by, by), 4)
    d["x"], d["seed"] = x.astype(BF), same(s.astype(BF))
    return d
def setup_inputs_late(rng):
    d = setup_inputs(rng)
    top = (np.arange(128) < 64)[:, None]
    a = np.stack([rng.permutation(C) < C // 2 for i in range(16 * N)]).reshape(N, 1, P)
    a = np.repeat(a, 4, axis=2)
    v = sizes(rng, N, 128, 4 * P)
    d["x"] = np.where(top, np.where(a, -np.abs(v), v * np.float32(2.0 ** -6)), np.where(a, 0, v)).astype(BF)
    d["seed"] = same(np.where(top, np.abs(sizes(rng, 128, 64)), 0).astype(BF))
    return d
def setup_inputs_one(rng):
    d = setup_inputs(rng)
    h = int(rng.integers(0, N))
    s = sizes(rng, 128, 64).astype(BF)
    d["seed"] = same(s)
    d["x"] = same(np.repeat(s.reshape(128, 16, 1, 4), C, axis=2).reshape(128, 4 * P))
    d["x"][h] = (sizes(rng, 128, 4 * P) * np.float32(2.0 ** -6)).astype(BF)
    return d
def setup_inputs_spread(rng):
    d = setup_inputs(rng)
    x, s = wide(rng, N, 128, 4 * P, cols=6).astype(np.float32), wide(rng, 128, 64).astype(np.float32)
    plus = rng.permutation(16) < 4
    x = np.where(np.repeat(plus, 4 * C), np.abs(x), x)
    s = np.where(np.repeat(plus, 4), np.abs(s), s)
    for b in np.flatnonzero(plus):
        for r, zero in zip(np.sort(rng.permutation(N)[:2]), (0.0, -0.0)):
            j = int(b * C + rng.integers(0, C))
            x[r, :, 4 * j:4 * j + 4] = np.float32(zero)
    d["x"], d["seed"] = x.astype(BF), same(s.astype(BF))
    return d
def setup_inputs_ties(rng):
    d = setup_inputs(rng)
    v = rng.standard_normal((128, 16, 12, 4), dtype=np.float32)
    v[:64, 1::2, 1::2] = v[:64, 1::2, ::2]
    s = rng.standard_normal((128, 16, 4), dtype=np.float32)
    s[64:, 1::2] = 0
    x = np.zeros((N, 128, 16, C, 4), np.float32)
    for b in range(16):
        own = np.stack([rng.permutation(N) < N // 2 for i in range(12)])
        own[1] = ~own[0]
        for r in range(N):
            e = rng.permutation(np.resize(np.flatnonzero(own[:, r]), C))
            x[r][:, b] = v[:, b][:, e]
    d["x"] = mx_ref.flush(x.reshape(N, 128, 4 * P).astype(BF))
    d["seed"] = same(mx_ref.flush(s.reshape(128, 64).astype(BF)))
    return d
def check_inputs(d):
    b = []
    for k in ("x", "seed", "w"):
        v = np.abs(d[k].astype(np.float32))
        if not (np.isfinite(v).all() and ((v == 0) | (v >= 2.0 ** -30) & (v <= 2.0 ** 30)).all()): b.append("a value of " + k)
    s = d["seed"].astype(np.float32)
    if not (s == s[:1]).all(): b.append("seed isn't the same on all ranks")
    return b
def reference(x, seed, w):
    q = [mx_ref.quantize(np.ascontiguousarray(x[r])) for r in range(N)]
    every = join(*q)
    c = mx_ref.quantize(np.ascontiguousarray(seed[0]))
    won, nb = [], np.zeros((R, 16), np.float32)
    for t in range(R):
        k = pick(c, np.concatenate([np.arange(16), np.full(112, -1)]))
        s = np.concatenate([mx_ref.matmul(k, v)[:16] for v in q], axis=1)
        s = s[CLOUD, np.arange(N * P)] + np.float32(0)
        m = s if t == 0 else np.maximum(m, s)
        e = []
        for b in range(16):
            i = np.flatnonzero(CLOUD == b)
            e.append(int(i[np.argmin(m[i])]))
        c = pick(every, np.array(e))
        won.append(c)
        nb[t] = e
    u = join(*won)
    oc, osc = emit(u)
    y = np.stack([np.concatenate([mx_ref.matmul(mx_ref.quantize(np.ascontiguousarray(cut(w[r], o))), u) for o in range(O)], axis=1) for r in range(N)])
    return {"oc": same(oc), "osc": same(osc), "nb": same(nb), "y": y}

@@ -1,0 +1,461 @@
+from concourse.bass import DstId, RemoteDMATransfer
+from concourse.mybir import dt, AluOpType, AxisListType, ActivationFunctionType
+
+P, R = 512, 4
+NB = 16
+L = 128
+H = 256
+D0 = 128
+KON = 4
+BIG = 8192
+
+SCRATCH = {
+    "xt": ("sbuf", [128, 4 * P], "bfloat16"),
+    "sd": ("sbuf", [128, 640], "bfloat16"),
+    "wt": ("sbuf", [128, 512], "bfloat16"),
+    "xqc": ("sbuf", [128, P], "float8_e4m3fn_x4"),
+    "xqs": ("sbuf", [128, P], "uint8"),
+    "xic": ("sbuf", [128, P], "float8_e4m3fn_x4"),
+    "xis": ("sbuf", [128, P], "uint8"),
+    "wqc": ("sbuf", [128, 128], "float8_e4m3fn_x4"),
+    "wqs": ("sbuf", [128, 128], "uint8"),
+    "dc": ("sbuf", [128, 640], "float8_e4m3fn_x4"),
+    "ds": ("sbuf", [128, 640], "uint8"),
+    "clc": ("sbuf", [128, 128], "float8_e4m3fn_x4"),
+    "cls": ("sbuf", [128, 128], "uint8"),
+    "cdc": ("sbuf", [128, 64], "float8_e4m3fn_x4"),
+    "cds": ("sbuf", [128, 64], "uint8"),
+    "cwc": ("sbuf", [128, 128], "float8_e4m3fn_x4"),
+    "cws": ("sbuf", [128, 128], "uint8"),
+    "mk": ("sbuf", [128, 32], "float32"),
+    "mn": ("sbuf", [128, 32], "float32"),
+    "msg": ("sbuf", [128, 1], "float32"),
+    "wmk": ("sbuf", [128, 4], "float32"),
+    "nbl": ("sbuf", [128, 1], "float32"),
+    "nbo": ("sbuf", [128, 1], "float32"),
+    "m": ("sbuf", [128, L], "float32"),
+    "mi": ("sbuf", [128, L], "float32"),
+    "pm": ("sbuf", [128, L * R], "float32"),
+    "sg": ("sbuf", [128, L], "bfloat16"),
+    "acc": ("sbuf", [128, 4], "float32"),
+    "uu": ("sbuf", [128, 4], "float32"),
+    "mz": ("sbuf", [128, 8], "float32"),
+    "ma": ("sbuf", [128, 8], "float32"),
+    "ml": ("sbuf", [128, 1], "float32"),
+    "acc8": ("sbuf", [128, 1], "float32"),
+    "u8": ("sbuf", [128, 2], "float32"),
+    "pm8": ("sbuf", [128, 8], "float32"),
+    "sg8": ("sbuf", [128, 8], "bfloat16"),
+    "pen": ("sbuf", [128, 8], "float32"),
+    "vv": ("sbuf", [128, 8], "float32"),
+    "offx": ("sbuf", [128, 8], "uint16"),
+    "offh": ("sbuf", [128, 2], "uint16"),
+    "io16": ("sbuf", [128, 2], "uint16"),
+    "xl": ("sbuf", [128, 32], "uint16"),
+    "pi": ("sbuf", [128, 1], "int32"),
+    "p15": ("sbuf", [128, 1], "int32"),
+    "p96": ("sbuf", [128, 1], "int32"),
+    "p12": ("sbuf", [128, 1], "int32"),
+    "p3": ("sbuf", [128, 1], "int32"),
+    "p16": ("sbuf", [128, 1], "int32"),
+    "p112": ("sbuf", [128, 1], "int32"),
+    "f15": ("sbuf", [128, 1], "float32"),
+    "so": ("sbuf", [128, 1], "float32"),
+    "va": ("sbuf", [128, L], "float32"),
+    "vb": ("sbuf", [128, L], "float32"),
+    "vl": ("sbuf", [128, 32], "float32"),
+    "f3": ("sbuf", [128, 1], "float32"),
+    "fl": ("sbuf", [128, 1], "float32"),
+    "bfd": ("sbuf", [128, 2], "float32"),
+    "bx1": ("sbuf", [128, 1], "float32"),
+    "bx2": ("sbuf", [128, 1], "float32"),
+    "br1": ("sbuf", [128, 1], "float32"),
+    "br2": ("sbuf", [128, 1], "float32"),
+    "bb1": ("sbuf", [128, 1], "float32"),
+    "bb2": ("sbuf", [128, 1], "float32"),
+    "ge0": ("sbuf", [128, 1], "float32"),
+    "val": ("sbuf", [128, 1], "float32"),
+    "hh": ("sbuf", [128, 1], "float32"),
+    "hl": ("sbuf", [128, 1], "float32"),
+    "nh": ("sbuf", [128, 1], "float32"),
+    "ch": ("sbuf", [128, 1], "float32"),
+    "f112": ("sbuf", [128, 1], "float32"),
+    "g3": ("sbuf", [128, 1], "float32"),
+    "qn": ("sbuf", [128, 4], "float32"),
+    "nv": ("sbuf", [128, 4], "float32"),
+    "zn": ("sbuf", [128, 4], "float32"),
+    "wn": ("sbuf", [128, 4], "float32"),
+    "en": ("sbuf", [128, 1], "float32"),
+    "e3": ("sbuf", [128, 1], "float32"),
+    "ys": ("sbuf", [128, 64], "float32"),
+    "ps": ("psum", [128, 2048], "float32"),
+    "psi": ("psum", [128, 512], "float32"),
+    "psy": ("psum", [128, 512], "float32"),
+}
+_ROUND = ["mm", "mx", "sc", "sg", "ua", "of", "xc", "xs", "ac", "as", "wm", "qn", "nv", "pk", "pl"]
+SEMAPHORES = (["%s%d" % (k, t) for k in _ROUND for t in range(1, R + 1)]
+              + ["lsd", "lx0", "lx1", "lw", "zs", "sd2", "qz0", "qsd", "qz2", "qz", "qcl", "qx0", "qx1", "qx2", "qw",
+                 "ipi", "iva", "ivb", "ivl", "ipt", "ip2", "f15", "so", "mask", "maski", "bx1", "bx2", "br", "bb", "ge0", "val",
+                 "bfd", "io16", "f3", "fl", "xl", "xic", "xis", "mmi", "mxi", "hh", "hl", "nh", "ch", "f112", "g3", "zmsg",
+                 "zpen", "hm", "hc", "hs", "hn", "mkc", "mza", "mzb", "ml", "s8", "sg8", "u8", "o8", "pc", "ps", "pen", "mnc",
+                 "vv", "nbo", "nbl", "z12", "w12", "e12", "m12", "z3", "w3", "e3", "msg", "my", "yc", "out", "loc"])
+
+
+def rank_program(g, core, T, topo):
+    me = T.rank_of(core)
+    if me is None:
+        return
+    A, X, F = AluOpType, AxisListType.X, ActivationFunctionType
+    cores = list(T.cores)
+    V, S, E, Y = g.vector, g.scalar, g.tensor, g.sync
+
+    def near(a, b):
+        return cores[b] in topo.cores_of(cores[a])
+
+    def linked(a, b):
+        return topo.mates(cores[a], cores[b]) or topo.same_plane(cores[a], cores[b])
+
+    def same_die(a, b):
+        return topo.die(cores[a]) == topo.die(cores[b])
+
+    pairs = [(a, b) for a in range(8) for b in range(a + 1, 8)
+             if not near(a, b) and not linked(a, b) and not same_die(a, b)]
+    my_round = [t for t in range(1, R + 1) if me in pairs[t - 1]][0]
+
+    def engines(a, b):
+        if not near(a, b):
+            return topo.engines(cores[a], cores[b])
+        far = [c for c in range(8) if not near(a, c)][0]
+        off = topo.engines(cores[a], cores[far])
+        return [e for e in topo.engines(cores[a], cores[b]) if e not in off][:KON]
+
+    def served(h, pair):
+        return [d for d in range(8) if d not in pair and (near(h, d) or linked(h, d) and same_die(h, d))]
+
+    need, waited = {}, set()
+
+    def ev(ins, name, n=1):
+        ins.then_inc(T.sem[name], n)
+        need[name] = n
+
+    def evs(calls, name):
+        for ins in calls:
+            ins.then_inc(T.sem[name], 1)
+        need[name] = len(calls)
+
+    def W(q, *names):
+        for k in names:
+            q.wait_ge(T.sem[k], need[k])
+            waited.add(k)
+
+    local = [0]
+
+    def send(src, dst, dests, sem):
+        trs = []
+        for group in ([d for d in dests if not near(me, d)], [d for d in dests if near(me, d)]):
+            if not group:
+                continue
+            es = engines(me, group[0])
+            ids = []
+            for d in group:
+                rid, pid = topo.addr(cores[d], core)
+                ids.append(DstId(rid=rid, pnc=pid))
+            trs.append(RemoteDMATransfer(dst_ids=ids, dma_engine_mask=sum(1 << e for e in es), remote_sem=T.sem[sem],
+                                         srcs=[src], dsts=[dst for _ in group]))
+            local[0] += len(es)
+        g.remote_dma_fused(trs, local_sem=T.sem.loc)
+
+    n7 = sum(len(engines(s, me)) for s in range(8) if s != me)
+    for k in ("hm", "hc", "hs") + (("hn",) if my_round == R else ()):
+        need[k] = n7
+    for t in range(1, R + 1):
+        if t != my_round:
+            h = [h for h in pairs[t - 1] if me in served(h, pairs[t - 1])][0]
+            for k in ("ac%d", "as%d") + (("wm%d",) if t < R else ()):
+                need[k % t] = len(engines(h, me))
+            if t == R:
+                need["nbl"] = len(engines(h, me))
+
+    def quarter(q):
+        return slice(32 * q, 32 * q + 32)
+
+    def at(t):
+        return D0 + 128 * (t - 1)
+
+    ev(Y.dma_start(T.xt[:, 0:4 * H], T.x[:, 0:4 * H]), "lx0", 16)
+    ev(S.dma_start(T.sd[:, 0:64], T.seed[:]), "lsd", 16)
+    ev(S.dma_start(T.xt[:, 4 * H:8 * H], T.x[:, 4 * H:8 * H]), "lx1", 16)
+    W(Y, "lx1")
+    ev(Y.dma_start(T.wt[:], T.w[:]), "lw", 16)
+
+    zeros = T.sd[:, 128:640]
+    ev(g.iota(T.pi[:], [[0, 1]], 0, 1), "ipi")
+    ev(g.iota(T.va[:], [[1, 4], [0, 32]], 0, 0, allow_small_or_imprecise_dtypes=True), "iva")
+    ev(g.iota(T.vl[:], [[128, 4], [4, 8]], 0, 0, allow_small_or_imprecise_dtypes=True), "ivl")
+    ev(g.iota(T.vb[:], [[0, 32], [1, 4]], 0, 0, allow_small_or_imprecise_dtypes=True), "ivb")
+    ev(V.memset(zeros, 0.0), "zs")
+    W(V, "ipi")
+    evs([V.tensor_scalar(T[b][:], T.pi[:], k, None, A.bitwise_and)
+         for b, k in (("p15", 15), ("p96", 96), ("p12", 12), ("p3", 3))], "ipt")
+    W(V, "zs")
+    ev(V.quantize_mx(T.dc[:, 0:128], T.ds[:, 0:128], zeros), "qz0")
+    W(V, "ipt")
+    ev(V.tensor_copy(T.f15[:], T.p15[:]), "f15")
+    ev(V.tensor_scalar(T.bx1[:], T.p12[:], 32.0, None, A.mult), "bx1")
+    ev(V.tensor_scalar(T.f3[:], T.p3[:], 32.0, None, A.mult), "f3")
+    W(V, "f15")
+    ev(V.tensor_scalar(T.so[:], T.p96[:], -0.125, T.f15[:, 0:1], A.mult, A.add), "so")
+    W(V, "so", "iva")
+    ev(V.tensor_scalar(T.m[:], T.va[:], T.so[:, 0:1], 1e29, A.not_equal, A.mult), "mask")
+    W(V, "lsd")
+    ev(V.tensor_copy(T.sd[:, 64:128], T.sd[:, 0:64]), "sd2")
+    W(V, "sd2")
+    ev(V.quantize_mx(T.dc[:, D0:D0 + 128], T.ds[:, D0:D0 + 128], T.sd[:, 0:512]), "qsd")
+    for j, (a, b) in enumerate(((0, H), (H, H + L), (H + L, P))):
+        W(V, "lx%d" % min(j, 1))
+        ev(V.quantize_mx(T.xqc[:, a:b], T.xqs[:, a:b], T.xt[:, 4 * a:4 * b]), "qx%d" % j)
+    W(V, "mask")
+    need["mask"] = 2
+    V.tensor_scalar(T.m[:], T.m[:], 5e28, None, A.subtract).then_inc(T.sem.mask, 1)
+    ev(V.quantize_mx(T.dc[:, at(2):at(3)], T.ds[:, at(2):at(3)], zeros), "qz2")
+    W(V, "mask")
+
+    def pm(t, a, b, s=1):
+        return T.pm[:, L * (t - 1) + a:L * (t - 1) + b:s]
+
+    def last(t):
+        return pm(t, L - 1, L)
+
+    def product(bank, t, xc, xs, name, waits):
+        for k in range(4):
+            W(E, *waits[k])
+            a = at(t) - 32 * k
+            ins = E.matmul_mx(bank, T.dc[:, a:a + 128], T.ds[:, a:a + 128],
+                              xc[:, L * k:L * k + L], xs[:, L * k:L * k + L], k == 0, k == 3)
+        ev(ins, name)
+
+    def candidate(t):
+        W(V, "sg%d" % t, "bb")
+        ev(V.tensor_scalar(T.qn[:, t - 1:t], T.acc[:, t - 1:t], (T.bb1 if t == 1 else T.bb2)[:, 0:1], None, A.add), "qn%d" % t)
+
+    def numbers(t):
+        if t == my_round:
+            W(V, "s8")
+            wm = T.pm8[:, 7:8]
+        else:
+            W(V, "wm%d" % t)
+            wm = T.wmk[:, t - 1:t]
+        W(V, "qn%d" % t)
+        ev(V.tensor_scalar(T.nv[:, t - 1:t], last(t), wm, T.qn[:, t - 1:t], A.is_equal, A.mult), "nv%d" % t)
+
+    for t in range(1, R + 1):
+        pair, hub = pairs[t - 1], t == my_round
+        n = str(t)
+        bank = T.ps[:, 512 * (t - 1):512 * (t - 1) + L]
+        if t == 1:
+            product(bank, 1, T.xqc, T.xqs, "mm1", [["qz0", "qsd", "qx0"], [], ["qx1"], ["qx2"]])
+        else:
+            here = ["pc", "ps"] if t - 1 == my_round else ["ac%d" % (t - 1), "as%d" % (t - 1)]
+            product(bank, t, T.xic, T.xis, "mm" + n, [here + ["qz2" if t == 2 else "qz"], [], [], []])
+        marks = T.m if t == 1 else T.mi
+        if t == 2:
+            W(V, "mxi")
+        W(V, "mm" + n)
+        ev(V.tensor_tensor(marks[:], bank, marks[:], A.max), "mx" + n)
+        W(V, "mx" + n)
+        ev(V.tensor_tensor_scan(pm(t, 0, L), marks[:], marks[:], 9e29, A.min, A.min), "sc" + n)
+        W(S, "sc" + n)
+        if t == 1:
+            ev(S.activation(T.sg[:], pm(t, 0, L), F.Sign, bias=last(t), scale=-1.0, accum_out=T.acc[:, 0:1]), "sg1")
+        else:
+            ev(S.activation(T.sg[:, 0:32], pm(t, 3, L, 4), F.Sign, bias=last(t), scale=-1.0, accum_out=T.acc[:, t - 1:t]), "sg" + n)
+        hubs = [h for h in pair if h != me]
+        W(g, "sc" + n)
+        send(last(t), T.mk[:, 4 * me:4 * me + 1], hubs, "hm")
+        W(V, "sg" + n, "bx1" if t == 1 else "bx2")
+        ev(V.tensor_scalar(T.uu[0:64, t - 1:t], T.acc[0:64, t - 1:t], -1.0, T.acc[64:128, t - 1:t], A.mult, A.subtract), "ua" + n)
+        W(V, "ua" + n)
+        bx = T.bx1 if t == 1 else T.bx2
+        o = 2 * (t - 1)
+        evs([V.tensor_scalar(T.offx[quarter(q), o:o + 1], T.uu[quarter(0), t - 1:t], T.uu[quarter(1), t - 1:t],
+                             bx[quarter(q), 0:1], A.add, A.add) for q in range(4)], "of" + n)
+        offx = T.offx[:, o:o + 1]
+        if hub:
+            cc, cs = T.cwc[:, NB * me:NB * me + NB], T.cws[:, NB * me:NB * me + NB]
+        else:
+            cc, cs = T.cdc[:, NB * (t - 1):NB * t], T.cds[:, NB * (t - 1):NB * t]
+        W(V, "of" + n, "qx0", "qx1", "qx2", *(["qz2"] if t == 1 else ["qz", "qcl"] if t == 2 else []))
+        ev(V.tensor_copy(cc.bitcast(dt.uint32), T.xqc[:, 0:P].bitcast(dt.uint32).indirect(offx)), "xc" + n)
+        W(S, "of" + n, "qx0", "qx1", "qx2")
+        ev(S.activation(cs, T.xqs[:, 0:P].indirect(offx), F.Copy), "xs" + n)
+        W(g, "xc" + n)
+        send(cc.bitcast(dt.uint8), T.cwc[:, NB * me:NB * me + NB].bitcast(dt.uint8), hubs, "hc")
+        W(g, "xs" + n)
+        send(cs, T.cws[:, NB * me:NB * me + NB], hubs, "hs")
+        if t == 1:
+            evs([V.tensor_scalar(T.bfd[0:32, j:j + 1], T.f15[0:32, :], 0.0625, None, A.mult) for j in range(2)]
+                + [V.memset(T.bfd[32:64, :], 0.0)], "bfd")
+            W(V, "f3")
+            ev(V.tensor_scalar(T.fl[:], T.p12[:], 0.25, T.f3[:, 0:1], A.mult, A.add), "fl")
+            W(V, "fl", "ivl")
+            ev(V.tensor_scalar(T.xl[:], T.vl[:], T.fl[:, 0:1], None, A.add), "xl")
+        if t == R:
+            W(V, "nh", "e3", "zmsg")
+            ev(V.tensor_scalar(T.msg[32:64, :], T.offx[32:64, o:o + 1], T.nh[32:64, 0:1], T.e3[32:64, 0:1], A.mult, A.add), "msg")
+            W(g, "msg", "m12", "zmsg")
+            send(T.msg[:], T.mn[:, 4 * me:4 * me + 1], hubs, "hn")
+
+        if hub:
+            ev(V.tensor_copy(T.mk[:, 4 * me:4 * me + 1], last(t)), "mkc")
+            W(V, "hm", "mkc")
+            ev(V.tensor_tensor_scan(T.pm8[:], T.mk[:, 0:32:4], T.mk[:, 0:32:4], 9e29, A.min, A.min), "s8")
+            W(S, "s8")
+            ev(S.activation(T.sg8[:], T.pm8[:], F.Sign, bias=T.pm8[:, 7:8], scale=-1.0, accum_out=T.acc8[:]), "sg8")
+            dests = served(me, pair)
+            if t == R - 1:
+                W(g, "s8")
+                send(T.pm8[:, 7:8], T.wmk[:, t - 1:t], dests, "wm" + n)
+            W(V, "sg8", "bfd")
+            ev(V.tensor_scalar(T.u8[0:64, :], T.bfd[0:64, :], T.acc8[0:64, 0:1], T.acc8[64:128, 0:1], A.subtract, A.subtract), "u8")
+            W(V, "u8")
+            evs([V.tensor_scalar(T.offh[quarter(q), :], T.u8[0:32, :], T.u8[32:64, 0:1], 16.0, A.add, A.mult)
+                 for q in range(4)], "o8")
+            if t < R:
+                a, k = at(t + 1), 2
+                wc, ws, zero = T.dc[:, a:a + 32], T.ds[:, a:a + 32], ("qz2" if t == 1 else "qz")
+            else:
+                k = 1
+                wc, ws, zero = T.clc[:, 48:64], T.cls[:, 48:64], "qcl"
+            W(V, "hc", "o8", "xc" + n, zero)
+            ev(V.tensor_copy(wc.bitcast(dt.uint32), T.cwc[:].bitcast(dt.uint32).indirect(T.offh[:, 0:k])), "pc")
+            W(S, "hs", "o8", "xs" + n, zero)
+            ev(S.activation(ws, T.cws[:].indirect(T.offh[:, 0:k]), F.Copy), "ps")
+            W(g, "pc")
+            send(wc.bitcast(dt.uint8), wc.bitcast(dt.uint8), dests, "ac" + n)
+            W(g, "ps")
+            send(ws, ws, dests, "as" + n)
+            if t < R - 1:
+                W(g, "s8")
+                send(T.pm8[:, 7:8], T.wmk[:, t - 1:t], dests, "wm" + n)
+            if t == R:
+                ev(V.tensor_tensor(T.mz[0:64, :], T.mk[0:64, 0:32:4], T.mk[64:128, 0:32:4], A.min), "mza")
+                W(V, "mza")
+                ev(V.tensor_tensor(T.ma[32:64, :], T.mz[0:32, :], T.mz[32:64, :], A.min), "mzb")
+                W(V, "mzb")
+                ev(V.tensor_reduce(T.ml[32:64, :], T.ma[32:64, :], X, A.min), "ml")
+                W(V, "ml", "g3", "zpen")
+                ev(V.tensor_scalar(T.pen[32:64, :], T.ma[32:64, :], T.ml[32:64, 0:1], T.g3[32:64, 0:1], A.not_equal, A.mult), "pen")
+                W(V, "msg", "m12", "zmsg")
+                ev(V.tensor_copy(T.mn[:, 4 * me:4 * me + 1], T.msg[:]), "mnc")
+                W(V, "pen", "mnc", "hn")
+                ev(V.tensor_tensor(T.vv[:], T.mn[:, 0:32:4], T.pen[:], A.add), "vv")
+                W(V, "vv")
+                ev(V.tensor_reduce(T.nbo[:], T.vv[:], X, A.max, negate=True), "nbo")
+                W(g, "nbo")
+                send(T.nbo[:], T.nbl[:], dests, "nbl")
+
+        if t == 1:
+            W(V, "xl")
+            ev(V.tensor_copy(T.xic[:].bitcast(dt.uint32), T.xqc[:].bitcast(dt.uint32).indirect(T.xl[:])), "xic")
+            W(S, "xl")
+            ev(S.activation(T.xis[:], T.xqs[:].indirect(T.xl[:]), F.Copy), "xis")
+            product(T.psi[:, 0:L], 1, T.xic, T.xis, "mmi", [["xic", "xis"], [], [], []])
+            W(V, "ivb", "so")
+            ev(V.tensor_scalar(T.mi[:], T.vb[:], T.so[:, 0:1], 1e29, A.not_equal, A.mult), "maski")
+            ev(V.tensor_scalar(T.bx2[:], T.f15[:], 32.0, None, A.mult), "bx2")
+            evs([V.quantize_mx(T.dc[:, a:a + 128], T.ds[:, a:a + 128], zeros) for a in (at(3), at(4))], "qz")
+            W(V, "maski")
+            need["maski"] = 2
+            V.tensor_scalar(T.mi[:], T.mi[:], 5e28, None, A.subtract).then_inc(T.sem.maski, 1)
+            W(V, "maski", "mmi")
+            ev(V.tensor_tensor(T.mi[:], T.psi[:, 0:L], T.mi[:], A.max), "mxi")
+            ev(V.quantize_mx(T.clc[:], T.cls[:], zeros), "qcl")
+        if t == 2:
+            ev(V.tensor_copy(T.io16[:, 0:1], T.f15[:]), "io16")
+        if t > 1:
+            a, b = at(t), 16 * (t - 2)
+            here = ["pc", "ps"] if t - 1 == my_round else ["ac%d" % (t - 1), "as%d" % (t - 1)]
+            W(V, here[0], "io16", "qcl")
+            ev(V.tensor_copy(T.clc[:, b:b + 16].bitcast(dt.uint32), T.dc[:, a:a + 32].bitcast(dt.uint32).indirect(T.io16[:, 0:1])), "pk" + n)
+            W(S, here[1], "io16", "qcl")
+            ev(S.activation(T.cls[:, b:b + 16], T.ds[:, a:a + 32].indirect(T.io16[:, 0:1]), F.Copy), "pl" + n)
+        if t == 2:
+            W(V, "lw")
+            ev(V.quantize_mx(T.wqc[:], T.wqs[:], T.wt[:]), "qw")
+            evs([V.tensor_scalar(T[b][:], T.pi[:], k, None, A.bitwise_and) for b, k in (("p16", 16), ("p112", 112))], "ip2")
+            ev(V.tensor_scalar(T.ge0[:], T.so[:], 0.0, None, A.is_ge), "ge0")
+            W(V, "bx1", "bx2")
+            evs([V.tensor_scalar(T[b][:], T[x][:], -1.0, float(BIG - P * me), A.mult, A.add)
+                 for b, x in (("br1", "bx1"), ("br2", "bx2"))], "br")
+            W(V, "ip2")
+            ev(V.tensor_scalar(T.hh[:], T.p16[:], 0.0625, None, A.mult), "hh")
+            ev(V.tensor_copy(T.f112[:], T.p112[:]), "f112")
+            W(V, "ge0")
+            ev(V.tensor_scalar(T.val[:], T.so[:], 3.0, T.ge0[:, 0:1], A.is_le, A.mult), "val")
+            ev(V.memset(T.msg[64:128, :], 0.0), "zmsg")
+            ev(V.memset(T.pen[:], 0.0), "zpen")
+            W(V, "hh", "f112")
+            ev(V.tensor_scalar(T.hl[:], T.hh[:], -1.0, 1.0, A.mult, A.add), "hl")
+            ev(V.tensor_scalar(T.nh[:], T.hh[:], -1.0, None, A.mult), "nh")
+            ev(V.tensor_scalar(T.ch[:], T.hh[:], float(BIG - P * me), float(BIG), A.mult, A.subtract), "ch")
+            ev(V.tensor_scalar(T.g3[:], T.f112[:], 48.0, -2.0 * BIG, A.is_equal, A.mult), "g3")
+            W(V, "val", "br")
+            evs([V.tensor_scalar(T[b][:], T[x][:], T.val[:, 0:1], None, A.mult)
+                 for b, x in (("bb1", "br1"), ("bb2", "br2"))], "bb")
+        if t == 3:
+            for k in range(1, 4):
+                candidate(k)
+            numbers(1)
+            numbers(2)
+            W(V, "nv1", "nv2")
+            ev(V.tensor_tensor(T.zn[0:64, 0:2], T.nv[0:64, 0:2], T.nv[64:128, 0:2], A.max), "z12")
+            W(V, "z12")
+            ev(V.tensor_tensor(T.wn[0:32, 0:2], T.zn[0:32, 0:2], T.zn[32:64, 0:2], A.max), "w12")
+            W(V, "w12", "hl")
+            ev(V.tensor_scalar(T.en[0:32, :], T.wn[0:32, 0:1], T.hl[0:32, 0:1], float(BIG), A.mult, A.subtract), "e12")
+            W(V, "e12")
+            ev(V.tensor_scalar(T.msg[0:32, :], T.wn[0:32, 1:2], T.hh[0:32, 0:1], T.en[0:32, 0:1], A.mult, A.add), "m12")
+            numbers(3)
+            W(V, "nv3")
+            ev(V.tensor_tensor(T.zn[0:64, 2:3], T.nv[0:64, 2:3], T.nv[64:128, 2:3], A.max), "z3")
+            W(V, "z3")
+            ev(V.tensor_scalar(T.wn[32:64, 2:3], T.zn[0:32, 2:3], T.zn[32:64, 2:3], T.hl[32:64, 0:1], A.max, A.mult), "w3")
+            W(V, "w3", "ch")
+            ev(V.tensor_scalar(T.e3[32:64, :], T.wn[32:64, 2:3], T.ch[32:64, 0:1], None, A.add), "e3")
+
+    if my_round == R:
+        cdone, sdone, ndone, nsrc = "pc", "ps", "nbo", T.nbo
+    else:
+        cdone, sdone, ndone, nsrc = "ac4", "as4", "nbl", T.nbl
+    pk, pl = ["pk2", "pk3", "pk4"], ["pl2", "pl3", "pl4"]
+    W(E, "qw", "qcl", *pk)
+    W(E, *pl)
+    W(E, cdone, sdone)
+    ev(E.matmul_mx(T.psy[:, 0:128], T.wqc[:], T.wqs[:], T.clc[:], T.cls[:], True, True), "my")
+    W(V, "my")
+    ev(V.tensor_copy(T.ys[:], T.psy[:, 0:64]), "yc")
+    outs = [0]
+
+    def store(q, a, b):
+        q.dma_start(a, b).then_inc(T.sem.out, 16)
+        outs[0] += 16
+
+    W(Y, *pk)
+    W(Y, cdone)
+    store(Y, T.oc[:], T.clc[:, 0:64].bitcast(dt.uint8))
+    W(Y, *pl)
+    W(Y, sdone)
+    store(Y, T.osc[0:4, :], T.cls[0:4, 0:64])
+    W(S, *pl)
+    W(S, sdone)
+    for k in range(1, 4):
+        store(S, T.osc[4 * k:4 * k + 4, :], T.cls[32 * k:32 * k + 4, 0:64])
+    W(Y, "yc")
+    store(Y, T.y[:], T.ys[:])
+    W(S, ndone)
+    store(S, T.nb[:], nsrc[0:64, 0:1])
+    g.wait_ge(T.sem.loc, local[0])
+    for k in sorted(need):
+        if k not in waited:
+            W(g, k)
+    g.wait_ge(T.sem.out, outs[0])

@@ -6,99 +6,46 @@ NB = 16
 L = 128
 H = 256
 D0 = 128
-KON = 4
+KON1 = (4, 8, 8, 8)
+KON2 = (8, 8, 8, 8)
+ALTERNATE = False
+AHEAD = (1, 2, 3)
 BIG = 8192
 
-SCRATCH = {
-    "xt": ("sbuf", [128, 4 * P], "bfloat16"),
-    "sd": ("sbuf", [128, 640], "bfloat16"),
-    "wt": ("sbuf", [128, 512], "bfloat16"),
-    "xqc": ("sbuf", [128, P], "float8_e4m3fn_x4"),
-    "xqs": ("sbuf", [128, P], "uint8"),
-    "xic": ("sbuf", [128, P], "float8_e4m3fn_x4"),
-    "xis": ("sbuf", [128, P], "uint8"),
-    "wqc": ("sbuf", [128, 128], "float8_e4m3fn_x4"),
-    "wqs": ("sbuf", [128, 128], "uint8"),
-    "dc": ("sbuf", [128, 640], "float8_e4m3fn_x4"),
-    "ds": ("sbuf", [128, 640], "uint8"),
-    "clc": ("sbuf", [128, 128], "float8_e4m3fn_x4"),
-    "cls": ("sbuf", [128, 128], "uint8"),
-    "cdc": ("sbuf", [128, 64], "float8_e4m3fn_x4"),
-    "cds": ("sbuf", [128, 64], "uint8"),
-    "cwc": ("sbuf", [128, 128], "float8_e4m3fn_x4"),
-    "cws": ("sbuf", [128, 128], "uint8"),
-    "mk": ("sbuf", [128, 32], "float32"),
-    "mn": ("sbuf", [128, 32], "float32"),
-    "msg": ("sbuf", [128, 1], "float32"),
-    "wmk": ("sbuf", [128, 4], "float32"),
-    "nbl": ("sbuf", [128, 1], "float32"),
-    "nbo": ("sbuf", [128, 1], "float32"),
-    "m": ("sbuf", [128, L], "float32"),
-    "mi": ("sbuf", [128, L], "float32"),
-    "pm": ("sbuf", [128, L * R], "float32"),
-    "sg": ("sbuf", [128, L], "bfloat16"),
-    "acc": ("sbuf", [128, 4], "float32"),
-    "uu": ("sbuf", [128, 4], "float32"),
-    "mz": ("sbuf", [128, 8], "float32"),
-    "ma": ("sbuf", [128, 8], "float32"),
-    "ml": ("sbuf", [128, 1], "float32"),
-    "acc8": ("sbuf", [128, 1], "float32"),
-    "u8": ("sbuf", [128, 2], "float32"),
-    "pm8": ("sbuf", [128, 8], "float32"),
-    "sg8": ("sbuf", [128, 8], "bfloat16"),
-    "pen": ("sbuf", [128, 8], "float32"),
-    "vv": ("sbuf", [128, 8], "float32"),
-    "offx": ("sbuf", [128, 8], "uint16"),
-    "offh": ("sbuf", [128, 2], "uint16"),
-    "io16": ("sbuf", [128, 2], "uint16"),
-    "xl": ("sbuf", [128, 32], "uint16"),
-    "pi": ("sbuf", [128, 1], "int32"),
-    "p15": ("sbuf", [128, 1], "int32"),
-    "p96": ("sbuf", [128, 1], "int32"),
-    "p12": ("sbuf", [128, 1], "int32"),
-    "p3": ("sbuf", [128, 1], "int32"),
-    "p16": ("sbuf", [128, 1], "int32"),
-    "p112": ("sbuf", [128, 1], "int32"),
-    "f15": ("sbuf", [128, 1], "float32"),
-    "so": ("sbuf", [128, 1], "float32"),
-    "va": ("sbuf", [128, L], "float32"),
-    "vb": ("sbuf", [128, L], "float32"),
-    "vl": ("sbuf", [128, 32], "float32"),
-    "f3": ("sbuf", [128, 1], "float32"),
-    "fl": ("sbuf", [128, 1], "float32"),
-    "bfd": ("sbuf", [128, 2], "float32"),
-    "bx1": ("sbuf", [128, 1], "float32"),
-    "bx2": ("sbuf", [128, 1], "float32"),
-    "br1": ("sbuf", [128, 1], "float32"),
-    "br2": ("sbuf", [128, 1], "float32"),
-    "bb1": ("sbuf", [128, 1], "float32"),
-    "bb2": ("sbuf", [128, 1], "float32"),
-    "ge0": ("sbuf", [128, 1], "float32"),
-    "val": ("sbuf", [128, 1], "float32"),
-    "hh": ("sbuf", [128, 1], "float32"),
-    "hl": ("sbuf", [128, 1], "float32"),
-    "nh": ("sbuf", [128, 1], "float32"),
-    "ch": ("sbuf", [128, 1], "float32"),
-    "f112": ("sbuf", [128, 1], "float32"),
-    "g3": ("sbuf", [128, 1], "float32"),
-    "qn": ("sbuf", [128, 4], "float32"),
-    "nv": ("sbuf", [128, 4], "float32"),
-    "zn": ("sbuf", [128, 4], "float32"),
-    "wn": ("sbuf", [128, 4], "float32"),
-    "en": ("sbuf", [128, 1], "float32"),
-    "e3": ("sbuf", [128, 1], "float32"),
-    "ys": ("sbuf", [128, 64], "float32"),
-    "ps": ("psum", [128, 2048], "float32"),
-    "psi": ("psum", [128, 512], "float32"),
-    "psy": ("psum", [128, 512], "float32"),
+C4, U8, F32, I32, U16, BF = "float8_e4m3fn_x4", "uint8", "float32", "int32", "uint16", "bfloat16"
+_SBUF = {
+    "xt": (4 * P, BF), "wt": (512, BF),
+    "sd": (640, BF),
+    "xqc": (P, C4), "xqs": (P, U8),
+    "xic": (P, C4), "xis": (P, U8),
+    "wqc": (128, C4), "wqs": (128, U8),
+    "dc": (640, C4), "ds": (640, U8),
+    "clc": (128, C4), "cls": (128, U8),
+    "cdc": (64, C4), "cds": (64, U8),
+    "cwc": (128, C4), "cws": (128, U8),
+    "mk": (32, F32),
+    "mn": (32, F32),
+    "msg": (1, F32),
+    "wmk": (16, F32),
+    "nbl": (1, F32),
+    "nbo": (1, F32), "m": (L, F32), "mi": (L, F32), "pm": (L * R, F32), "sg": (L, BF), "acc": (4, F32),
+    "acc8": (1, F32), "pm8": (8, F32), "sg8": (8, F32), "pen": (8, F32), "vv": (8, F32),
+    "offx": (8, U16), "offh": (2, U16), "io16": (2, U16), "xl": (32, U16),
+    "pi": (2, I32), "p15": (2, I32), "p96": (1, I32), "p12": (1, I32), "p16": (1, I32),
+    "f15": (1, F32), "so": (1, F32), "va": (L, F32), "vb": (L, F32), "vl": (32, F32), "fl": (1, F32),
+    "bfd": (2, F32), "bx1": (1, F32), "bx2": (1, F32),
+    "kn": (8, F32),
+    "en": (4, F32), "qn": (4, F32), "an": (2, F32), "ys": (64, F32),
 }
-_ROUND = ["mm", "mx", "sc", "sg", "ua", "of", "xc", "xs", "ac", "as", "wm", "qn", "nv", "pk", "pl"]
+SCRATCH = {k: ("sbuf", [128, n], d) for k, (n, d) in _SBUF.items()}
+SCRATCH.update({"ps": ("psum", [128, 2048], F32), "psi": ("psum", [128, 512], F32), "psy": ("psum", [128, 512], F32)})
+_ROUND = ["mm", "mx", "sc", "sg", "of", "xc", "xs", "ac", "as", "wm", "qn", "en", "nv", "pk", "pl"]
 SEMAPHORES = (["%s%d" % (k, t) for k in _ROUND for t in range(1, R + 1)]
-              + ["lsd", "lx0", "lx1", "lw", "zs", "sd2", "qz0", "qsd", "qz2", "qz", "qcl", "qx0", "qx1", "qx2", "qw",
-                 "ipi", "iva", "ivb", "ivl", "ipt", "ip2", "f15", "so", "mask", "maski", "bx1", "bx2", "br", "bb", "ge0", "val",
-                 "bfd", "io16", "f3", "fl", "xl", "xic", "xis", "mmi", "mxi", "hh", "hl", "nh", "ch", "f112", "g3", "zmsg",
-                 "zpen", "hm", "hc", "hs", "hn", "mkc", "mza", "mzb", "ml", "s8", "sg8", "u8", "o8", "pc", "ps", "pen", "mnc",
-                 "vv", "nbo", "nbl", "z12", "w12", "e12", "m12", "z3", "w3", "e3", "msg", "my", "yc", "out", "loc"])
+              + ["lsd", "lx0", "lx1", "lx2", "lw", "zs", "sd2", "qz1", "qsd", "qz2", "qz3", "qz4", "qcl", "qx0", "qx1", "qx2", "qw",
+                 "ipi", "iva", "ivb", "ivl", "ipt", "ip2", "f15", "so", "mask", "maski", "bx", "zpm", "zp8", "kn",
+                 "bfd", "io16", "fl", "xl", "xic0", "xis0", "xic1", "xis1", "mmi", "mxi", "zmsg",
+                 "zpen", "hm", "hc", "hs", "hn", "mkc", "s8", "sg8", "o8", "pc", "ps", "pen", "mnc",
+                 "vv", "nbo", "nbl", "msg", "my", "yc", "out", "loc", "wgo"])
 
 
 def rank_program(g, core, T, topo):
@@ -120,14 +67,20 @@ def rank_program(g, core, T, topo):
 
     pairs = [(a, b) for a in range(8) for b in range(a + 1, 8)
              if not near(a, b) and not linked(a, b) and not same_die(a, b)]
+    if ALTERNATE:
+        rest, pairs = pairs[1:], pairs[:1]
+        while rest:
+            nxt = [p for p in rest if not any(near(a, b) for a in p for b in pairs[-1])][0]
+            rest.remove(nxt)
+            pairs.append(nxt)
     my_round = [t for t in range(1, R + 1) if me in pairs[t - 1]][0]
 
-    def engines(a, b):
+    def engines(a, b, kon):
         if not near(a, b):
             return topo.engines(cores[a], cores[b])
         far = [c for c in range(8) if not near(a, c)][0]
         off = topo.engines(cores[a], cores[far])
-        return [e for e in topo.engines(cores[a], cores[b]) if e not in off][:KON]
+        return [e for e in topo.engines(cores[a], cores[b]) if e not in off][:kon]
 
     def served(h, pair):
         return [d for d in range(8) if d not in pair and (near(h, d) or linked(h, d) and same_die(h, d))]
@@ -148,83 +101,84 @@ def rank_program(g, core, T, topo):
             q.wait_ge(T.sem[k], need[k])
             waited.add(k)
 
-    local = [0]
+    need["loc"] = need["wgo"] = 0
 
-    def send(src, dst, dests, sem):
+    def send(src, dst, dests, sem, kon, local="loc"):
         trs = []
         for group in ([d for d in dests if not near(me, d)], [d for d in dests if near(me, d)]):
             if not group:
                 continue
-            es = engines(me, group[0])
+            es = engines(me, group[0], kon)
             ids = []
             for d in group:
                 rid, pid = topo.addr(cores[d], core)
                 ids.append(DstId(rid=rid, pnc=pid))
             trs.append(RemoteDMATransfer(dst_ids=ids, dma_engine_mask=sum(1 << e for e in es), remote_sem=T.sem[sem],
                                          srcs=[src], dsts=[dst for _ in group]))
-            local[0] += len(es)
-        g.remote_dma_fused(trs, local_sem=T.sem.loc)
+            need[local] += len(es)
+        g.remote_dma_fused(trs, local_sem=T.sem[local])
 
-    n7 = sum(len(engines(s, me)) for s in range(8) if s != me)
+    n7 = sum(len(engines(s, me, KON1[my_round - 1])) for s in range(8) if s != me)
     for k in ("hm", "hc", "hs") + (("hn",) if my_round == R else ()):
         need[k] = n7
     for t in range(1, R + 1):
         if t != my_round:
             h = [h for h in pairs[t - 1] if me in served(h, pairs[t - 1])][0]
-            for k in ("ac%d", "as%d") + (("wm%d",) if t < R else ()):
-                need[k % t] = len(engines(h, me))
-            if t == R:
-                need["nbl"] = len(engines(h, me))
+            for k in ("ac%d" % t, "as%d" % t, "wm%d" % t if t < R else "nbl"):
+                need[k] = len(engines(h, me, KON2[t - 1]))
 
     def quarter(q):
         return slice(32 * q, 32 * q + 32)
 
+    lo, hi = slice(0, 64), slice(64, 128)
+
     def at(t):
         return D0 + 128 * (t - 1)
 
-    ev(Y.dma_start(T.xt[:, 0:4 * H], T.x[:, 0:4 * H]), "lx0", 16)
-    ev(S.dma_start(T.sd[:, 0:64], T.seed[:]), "lsd", 16)
-    ev(S.dma_start(T.xt[:, 4 * H:8 * H], T.x[:, 4 * H:8 * H]), "lx1", 16)
-    W(Y, "lx1")
-    ev(Y.dma_start(T.wt[:], T.w[:]), "lw", 16)
+    parts = ((0, H), (H, H + L), (H + L, P))
+    ev(Y.dma_start(T.sd[:, 0:64], T.seed[:]), "lsd", 16)
+    for j, (a, b) in enumerate(parts):
+        ev(Y.dma_start(T.xt[:, 4 * a:4 * b], T.x[:, 4 * a:4 * b]), "lx%d" % j, 16)
 
     zeros = T.sd[:, 128:640]
-    ev(g.iota(T.pi[:], [[0, 1]], 0, 1), "ipi")
+
+    def zero(name, c, s, a):
+        ev(V.quantize_mx(c[:, a:a + 128], s[:, a:a + 128], zeros), name)
+
+    ev(g.iota(T.pi[:], [[0, 2]], 0, 1), "ipi")
     ev(g.iota(T.va[:], [[1, 4], [0, 32]], 0, 0, allow_small_or_imprecise_dtypes=True), "iva")
     ev(g.iota(T.vl[:], [[128, 4], [4, 8]], 0, 0, allow_small_or_imprecise_dtypes=True), "ivl")
     ev(g.iota(T.vb[:], [[0, 32], [1, 4]], 0, 0, allow_small_or_imprecise_dtypes=True), "ivb")
     ev(V.memset(zeros, 0.0), "zs")
     W(V, "ipi")
-    evs([V.tensor_scalar(T[b][:], T.pi[:], k, None, A.bitwise_and)
-         for b, k in (("p15", 15), ("p96", 96), ("p12", 12), ("p3", 3))], "ipt")
+    evs([V.tensor_scalar(T.p15[:], T.pi[:], 15, None, A.bitwise_and)]
+        + [V.tensor_scalar(T[b][:], T.pi[:, 0:1], k, None, A.bitwise_and) for b, k in (("p96", 96), ("p12", 12))], "ipt")
     W(V, "zs")
-    ev(V.quantize_mx(T.dc[:, 0:128], T.ds[:, 0:128], zeros), "qz0")
+    zero("qz1", T.dc, T.ds, 0)
     W(V, "ipt")
-    ev(V.tensor_copy(T.f15[:], T.p15[:]), "f15")
-    ev(V.tensor_scalar(T.bx1[:], T.p12[:], 32.0, None, A.mult), "bx1")
-    ev(V.tensor_scalar(T.f3[:], T.p3[:], 32.0, None, A.mult), "f3")
+    ev(V.tensor_copy(T.f15[:], T.p15[:, 0:1]), "f15")
+    evs([V.tensor_scalar(T.bx1[:], T.p12[:], 32.0, None, A.mult),
+         V.tensor_scalar(T.bx2[:], T.p15[:, 0:1], 32.0, None, A.mult)], "bx")
     W(V, "f15")
     ev(V.tensor_scalar(T.so[:], T.p96[:], -0.125, T.f15[:, 0:1], A.mult, A.add), "so")
+    ev(V.memset(T.pm[hi, L - 1:L * R:L], 0.0), "zpm")
     W(V, "so", "iva")
     ev(V.tensor_scalar(T.m[:], T.va[:], T.so[:, 0:1], 1e29, A.not_equal, A.mult), "mask")
     W(V, "lsd")
     ev(V.tensor_copy(T.sd[:, 64:128], T.sd[:, 0:64]), "sd2")
     W(V, "sd2")
     ev(V.quantize_mx(T.dc[:, D0:D0 + 128], T.ds[:, D0:D0 + 128], T.sd[:, 0:512]), "qsd")
-    for j, (a, b) in enumerate(((0, H), (H, H + L), (H + L, P))):
-        W(V, "lx%d" % min(j, 1))
+    W(V, "mask", "bx")
+    for j, (a, b) in enumerate(parts):
+        W(V, "lx%d" % j)
         ev(V.quantize_mx(T.xqc[:, a:b], T.xqs[:, a:b], T.xt[:, 4 * a:4 * b]), "qx%d" % j)
-    W(V, "mask")
-    need["mask"] = 2
-    V.tensor_scalar(T.m[:], T.m[:], 5e28, None, A.subtract).then_inc(T.sem.mask, 1)
-    ev(V.quantize_mx(T.dc[:, at(2):at(3)], T.ds[:, at(2):at(3)], zeros), "qz2")
-    W(V, "mask")
+    W(g, "zpm")
 
-    def pm(t, a, b, s=1):
-        return T.pm[:, L * (t - 1) + a:L * (t - 1) + b:s]
+    def pm(t, a, b, s=1, rows=slice(0, 128)):
+        return T.pm[rows, L * (t - 1) + a:L * (t - 1) + b:s]
 
-    def last(t):
-        return pm(t, L - 1, L)
+    def last(t, rows=slice(0, 128)):
+        return pm(t, L - 1, L, 1, rows)
 
     def product(bank, t, xc, xs, name, waits):
         for k in range(4):
@@ -234,194 +188,195 @@ def rank_program(g, core, T, topo):
                               xc[:, L * k:L * k + L], xs[:, L * k:L * k + L], k == 0, k == 3)
         ev(ins, name)
 
-    def candidate(t):
-        W(V, "sg%d" % t, "bb")
-        ev(V.tensor_scalar(T.qn[:, t - 1:t], T.acc[:, t - 1:t], (T.bb1 if t == 1 else T.bb2)[:, 0:1], None, A.add), "qn%d" % t)
+    def hub_constants():
+        ev(V.tensor_scalar(T.bfd[lo, :], T.p15[lo, :], 0.0625, None, A.mult), "bfd")
+        ev(V.memset(T.pm8[hi, :], 0.0), "zp8")
+
+    def alternate(j):
+        off = T.xl[:, 16 * j:16 * j + 16]
+        W(V, "xl")
+        ev(V.tensor_copy(T.xic[:, H * j:H * j + H].bitcast(dt.uint32), T.xqc[:].bitcast(dt.uint32).indirect(off)), "xic%d" % j)
+        W(S, "xl")
+        ev(S.activation(T.xis[:, H * j:H * j + H], T.xqs[:].indirect(off), F.Copy), "xis%d" % j)
+
+    def later_constants():
+        zero("qz4", T.dc, T.ds, at(4))
+        zero("qcl", T.clc, T.cls, 0)
+        ev(V.tensor_copy(T.io16[:, 0:1], T.f15[:]), "io16")
+        ev(V.tensor_scalar(T.p16[:], T.pi[:, 0:1], 16, None, A.bitwise_and), "ip2")
+        ev(V.memset(T.msg[hi, :], 0.0), "zmsg")
+        if my_round == R:
+            ev(V.memset(T.pen[:], 0.0), "zpen")
+        W(V, "ip2")
+        k = float(BIG - P * me)
+        evs([V.tensor_scalar(T.kn[lo, j:j + 1], T.p16[lo, :], a / 16, b, A.mult, A.add)
+             for j, (a, b) in enumerate(((1.0, -1.0), (-1.0, 0.0), (-k, k), (k, 0.0), (k, -float(BIG)), (2.0 * BIG, 0.0)))], "kn")
 
     def numbers(t):
+        q, h = quarter((t - 1) // 2), (t - 1) % 2
+        W(V, "kn")
+        ev(V.tensor_scalar(T.qn[q, t - 1:t], T.offx[q, 2 * t - 2:2 * t - 1], T.kn[q, h:h + 1], T.kn[q, 2 + h:3 + h], A.mult, A.add),
+           "qn%d" % t)
         if t == my_round:
-            W(V, "s8")
-            wm = T.pm8[:, 7:8]
+            wm = T.pm8[quarter(0), 7:8]
         else:
             W(V, "wm%d" % t)
-            wm = T.wmk[:, t - 1:t]
-        W(V, "qn%d" % t)
-        ev(V.tensor_scalar(T.nv[:, t - 1:t], last(t), wm, T.qn[:, t - 1:t], A.is_equal, A.mult), "nv%d" % t)
+            wm = T.wmk[quarter(0), 4 * t - 4:4 * t - 3]
+        ev(V.tensor_scalar(T.en[q, t - 1:t], last(t, quarter(0)), last(t, quarter(1)), wm, A.min, A.is_equal), "en%d" % t)
+        W(V, "qn%d" % t, "en%d" % t)
+        if t == 1:
+            ins = V.tensor_scalar(T.an[q, 0:1], T.en[q, 0:1], T.qn[q, 0:1], float(BIG), A.mult, A.subtract)
+        elif t == 2:
+            W(V, "nv1")
+            ins = V.tensor_scalar(T.msg[q, :], T.en[q, 1:2], T.qn[q, 1:2], T.an[q, 0:1], A.mult, A.add)
+        else:
+            ins = V.tensor_scalar(T.an[q, 1:2], T.en[q, 2:3], T.qn[q, 2:3], T.kn[q, 4:5], A.mult, A.add)
+        ev(ins, "nv%d" % t)
+
+    w_round = 2 if my_round == 1 else 1
+    qw_round = 3 if my_round <= 2 else 2
 
     for t in range(1, R + 1):
         pair, hub = pairs[t - 1], t == my_round
         n = str(t)
+        k1, k2 = KON1[t - 1], KON2[t - 1]
         bank = T.ps[:, 512 * (t - 1):512 * (t - 1) + L]
         if t == 1:
-            product(bank, 1, T.xqc, T.xqs, "mm1", [["qz0", "qsd", "qx0"], [], ["qx1"], ["qx2"]])
+            product(bank, 1, T.xqc, T.xqs, "mm1", [["qz1", "qsd", "qx0"], [], ["qx1"], ["qx2"]])
         else:
             here = ["pc", "ps"] if t - 1 == my_round else ["ac%d" % (t - 1), "as%d" % (t - 1)]
-            product(bank, t, T.xic, T.xis, "mm" + n, [here + ["qz2" if t == 2 else "qz"], [], [], []])
+            product(bank, t, T.xic, T.xis, "mm" + n, [["qz" + n] + here, [], [], []])
         marks = T.m if t == 1 else T.mi
         if t == 2:
             W(V, "mxi")
+        if t > 1:
+            W(V, "qz%d" % (t + 1) if t < R else "qcl")
         W(V, "mm" + n)
-        ev(V.tensor_tensor(marks[:], bank, marks[:], A.max), "mx" + n)
+        ev(V.tensor_tensor(marks[:], bank, marks[:], A.add if t == 1 else A.max), "mx" + n)
         W(V, "mx" + n)
-        ev(V.tensor_tensor_scan(pm(t, 0, L), marks[:], marks[:], 9e29, A.min, A.min), "sc" + n)
+        ev(V.tensor_tensor_scan(pm(t, 0, L, 1, lo), marks[lo, :], marks[hi, :], 9e29, A.min, A.min), "sc" + n)
         W(S, "sc" + n)
         if t == 1:
-            ev(S.activation(T.sg[:], pm(t, 0, L), F.Sign, bias=last(t), scale=-1.0, accum_out=T.acc[:, 0:1]), "sg1")
+            ev(S.activation(T.sg[lo, :], pm(t, 0, L, 1, lo), F.Sign, bias=last(t, lo), scale=-1.0,
+                            accum_out=T.acc[lo, 0:1]), "sg1")
+            W(V, "sc1")
+            zero("qz2", T.dc, T.ds, at(2))
         else:
-            ev(S.activation(T.sg[:, 0:32], pm(t, 3, L, 4), F.Sign, bias=last(t), scale=-1.0, accum_out=T.acc[:, t - 1:t]), "sg" + n)
+            ev(S.activation(T.sg[lo, 0:32], pm(t, 3, L, 4, lo), F.Sign, bias=last(t, lo), scale=-1.0,
+                            accum_out=T.acc[lo, t - 1:t]), "sg" + n)
         hubs = [h for h in pair if h != me]
         W(g, "sc" + n)
-        send(last(t), T.mk[:, 4 * me:4 * me + 1], hubs, "hm")
-        W(V, "sg" + n, "bx1" if t == 1 else "bx2")
-        ev(V.tensor_scalar(T.uu[0:64, t - 1:t], T.acc[0:64, t - 1:t], -1.0, T.acc[64:128, t - 1:t], A.mult, A.subtract), "ua" + n)
-        W(V, "ua" + n)
+        send(last(t), T.mk[:, 4 * me:4 * me + 1], hubs, "hm", k1)
+        W(V, "sg" + n)
         bx = T.bx1 if t == 1 else T.bx2
         o = 2 * (t - 1)
-        evs([V.tensor_scalar(T.offx[quarter(q), o:o + 1], T.uu[quarter(0), t - 1:t], T.uu[quarter(1), t - 1:t],
-                             bx[quarter(q), 0:1], A.add, A.add) for q in range(4)], "of" + n)
+        evs([V.tensor_scalar(T.offx[quarter(q), o:o + 1], bx[quarter(q), 0:1], T.acc[quarter(0), t - 1:t],
+                             T.acc[quarter(1), t - 1:t], A.subtract, A.subtract) for q in range(4)], "of" + n)
         offx = T.offx[:, o:o + 1]
         if hub:
             cc, cs = T.cwc[:, NB * me:NB * me + NB], T.cws[:, NB * me:NB * me + NB]
         else:
             cc, cs = T.cdc[:, NB * (t - 1):NB * t], T.cds[:, NB * (t - 1):NB * t]
-        W(V, "of" + n, "qx0", "qx1", "qx2", *(["qz2"] if t == 1 else ["qz", "qcl"] if t == 2 else []))
+        if t == 1:
+            W(V, "qz2")
+        W(V, "of" + n)
         ev(V.tensor_copy(cc.bitcast(dt.uint32), T.xqc[:, 0:P].bitcast(dt.uint32).indirect(offx)), "xc" + n)
-        W(S, "of" + n, "qx0", "qx1", "qx2")
+        W(S, "of" + n)
         ev(S.activation(cs, T.xqs[:, 0:P].indirect(offx), F.Copy), "xs" + n)
         W(g, "xc" + n)
-        send(cc.bitcast(dt.uint8), T.cwc[:, NB * me:NB * me + NB].bitcast(dt.uint8), hubs, "hc")
+        send(cc.bitcast(dt.uint8), T.cwc[:, NB * me:NB * me + NB].bitcast(dt.uint8), hubs, "hc", k1)
         W(g, "xs" + n)
-        send(cs, T.cws[:, NB * me:NB * me + NB], hubs, "hs")
+        send(cs, T.cws[:, NB * me:NB * me + NB], hubs, "hs", k1, "wgo" if t == w_round else "loc")
+        if t == R:
+            q = quarter(1)
+            W(V, "nv3", "zmsg")
+            ev(V.tensor_scalar(T.msg[q, :], T.offx[q, o:o + 1], T.kn[q, 1:2], T.an[q, 1:2], A.mult, A.add), "msg")
+            W(g, "msg", "nv2", "zmsg")
+            send(T.msg[:], T.mn[:, 4 * me:4 * me + 1], hubs, "hn", k1)
         if t == 1:
-            evs([V.tensor_scalar(T.bfd[0:32, j:j + 1], T.f15[0:32, :], 0.0625, None, A.mult) for j in range(2)]
-                + [V.memset(T.bfd[32:64, :], 0.0)], "bfd")
-            W(V, "f3")
-            ev(V.tensor_scalar(T.fl[:], T.p12[:], 0.25, T.f3[:, 0:1], A.mult, A.add), "fl")
+            if hub:
+                hub_constants()
+            ev(V.tensor_scalar(T.fl[:], T.p12[:], -31.75, T.bx2[:, 0:1], A.mult, A.add), "fl")
+        if hub:
+            ev(V.tensor_copy(T.mk[lo, 4 * me:4 * me + 1], last(t, lo)), "mkc")
+        if t == 1:
             W(V, "fl", "ivl")
             ev(V.tensor_scalar(T.xl[:], T.vl[:], T.fl[:, 0:1], None, A.add), "xl")
-        if t == R:
-            W(V, "nh", "e3", "zmsg")
-            ev(V.tensor_scalar(T.msg[32:64, :], T.offx[32:64, o:o + 1], T.nh[32:64, 0:1], T.e3[32:64, 0:1], A.mult, A.add), "msg")
-            W(g, "msg", "m12", "zmsg")
-            send(T.msg[:], T.mn[:, 4 * me:4 * me + 1], hubs, "hn")
+            alternate(0)
 
         if hub:
-            ev(V.tensor_copy(T.mk[:, 4 * me:4 * me + 1], last(t)), "mkc")
-            W(V, "hm", "mkc")
-            ev(V.tensor_tensor_scan(T.pm8[:], T.mk[:, 0:32:4], T.mk[:, 0:32:4], 9e29, A.min, A.min), "s8")
-            W(S, "s8")
-            ev(S.activation(T.sg8[:], T.pm8[:], F.Sign, bias=T.pm8[:, 7:8], scale=-1.0, accum_out=T.acc8[:]), "sg8")
+            if t == R:
+                W(V, "msg", "nv2", "zmsg")
+                ev(V.tensor_copy(T.mn[:, 4 * me:4 * me + 1], T.msg[:]), "mnc")
+            W(V, "mkc", "bfd", "xc" + n, "hm")
+            evs([V.tensor_tensor_scan(T.pm8[quarter(q), :], T.mk[quarter(0), 0:32:4], T.mk[quarter(1), 0:32:4], 9e29, A.min, A.min)
+                 for q in range(2)], "s8")
+            W(S, "qz%d" % (t + 1) if t < R else "qcl", "xs" + n, "s8")
+            ev(S.activation(T.sg8[lo, :], T.pm8[lo, :], F.Sign, bias=T.pm8[lo, 7:8], scale=-1.0, accum_out=T.acc8[lo, :]), "sg8")
             dests = served(me, pair)
-            if t == R - 1:
+            if t < R:
+                W(g, "zp8")
+            if t in AHEAD:
                 W(g, "s8")
-                send(T.pm8[:, 7:8], T.wmk[:, t - 1:t], dests, "wm" + n)
-            W(V, "sg8", "bfd")
-            ev(V.tensor_scalar(T.u8[0:64, :], T.bfd[0:64, :], T.acc8[0:64, 0:1], T.acc8[64:128, 0:1], A.subtract, A.subtract), "u8")
-            W(V, "u8")
-            evs([V.tensor_scalar(T.offh[quarter(q), :], T.u8[0:32, :], T.u8[32:64, 0:1], 16.0, A.add, A.mult)
-                 for q in range(4)], "o8")
+                send(T.pm8[:, 7:8], T.wmk[:, 4 * t - 4:4 * t - 3], dests, "wm" + n, k2)
+            W(V, "sg8")
+            evs([V.tensor_scalar(T.offh[half, :], T.bfd[lo, :], T.acc8[lo, 0:1], 16.0, A.subtract, A.mult)
+                 for half in (lo, hi)], "o8")
             if t < R:
                 a, k = at(t + 1), 2
-                wc, ws, zero = T.dc[:, a:a + 32], T.ds[:, a:a + 32], ("qz2" if t == 1 else "qz")
+                wc, ws = T.dc[:, a:a + 32], T.ds[:, a:a + 32]
             else:
                 k = 1
-                wc, ws, zero = T.clc[:, 48:64], T.cls[:, 48:64], "qcl"
-            W(V, "hc", "o8", "xc" + n, zero)
+                wc, ws = T.clc[:, 48:64], T.cls[:, 48:64]
+                W(S, "sg8", "kn", "zpen")
+                ev(S.activation(T.pen[quarter(1), :], T.sg8[quarter(1), :], F.Identity, scale=T.kn[quarter(1), 5:6]), "pen")
+            W(V, "o8", "hc")
             ev(V.tensor_copy(wc.bitcast(dt.uint32), T.cwc[:].bitcast(dt.uint32).indirect(T.offh[:, 0:k])), "pc")
-            W(S, "hs", "o8", "xs" + n, zero)
+            W(S, "o8", "hs")
             ev(S.activation(ws, T.cws[:].indirect(T.offh[:, 0:k]), F.Copy), "ps")
             W(g, "pc")
-            send(wc.bitcast(dt.uint8), wc.bitcast(dt.uint8), dests, "ac" + n)
+            send(wc.bitcast(dt.uint8), wc.bitcast(dt.uint8), dests, "ac" + n, k2)
             W(g, "ps")
-            send(ws, ws, dests, "as" + n)
-            if t < R - 1:
-                W(g, "s8")
-                send(T.pm8[:, 7:8], T.wmk[:, t - 1:t], dests, "wm" + n)
+            send(ws, ws, dests, "as" + n, k2)
+            if t < R and t not in AHEAD:
+                send(T.pm8[:, 7:8], T.wmk[:, 4 * t - 4:4 * t - 3], dests, "wm" + n, k2)
             if t == R:
-                ev(V.tensor_tensor(T.mz[0:64, :], T.mk[0:64, 0:32:4], T.mk[64:128, 0:32:4], A.min), "mza")
-                W(V, "mza")
-                ev(V.tensor_tensor(T.ma[32:64, :], T.mz[0:32, :], T.mz[32:64, :], A.min), "mzb")
-                W(V, "mzb")
-                ev(V.tensor_reduce(T.ml[32:64, :], T.ma[32:64, :], X, A.min), "ml")
-                W(V, "ml", "g3", "zpen")
-                ev(V.tensor_scalar(T.pen[32:64, :], T.ma[32:64, :], T.ml[32:64, 0:1], T.g3[32:64, 0:1], A.not_equal, A.mult), "pen")
-                W(V, "msg", "m12", "zmsg")
-                ev(V.tensor_copy(T.mn[:, 4 * me:4 * me + 1], T.msg[:]), "mnc")
                 W(V, "pen", "mnc", "hn")
                 ev(V.tensor_tensor(T.vv[:], T.mn[:, 0:32:4], T.pen[:], A.add), "vv")
                 W(V, "vv")
                 ev(V.tensor_reduce(T.nbo[:], T.vv[:], X, A.max, negate=True), "nbo")
                 W(g, "nbo")
-                send(T.nbo[:], T.nbl[:], dests, "nbl")
+                send(T.nbo[:], T.nbl[:], dests, "nbl", k2)
 
+        if t == w_round:
+            W(Y, "wgo")
+            ev(Y.dma_start(T.wt[:], T.w[:]), "lw", 16)
         if t == 1:
-            W(V, "xl")
-            ev(V.tensor_copy(T.xic[:].bitcast(dt.uint32), T.xqc[:].bitcast(dt.uint32).indirect(T.xl[:])), "xic")
-            W(S, "xl")
-            ev(S.activation(T.xis[:], T.xqs[:].indirect(T.xl[:]), F.Copy), "xis")
-            product(T.psi[:, 0:L], 1, T.xic, T.xis, "mmi", [["xic", "xis"], [], [], []])
+            alternate(1)
+            product(T.psi[:, 0:L], 1, T.xic, T.xis, "mmi", [["xic0", "xis0"], [], ["xic1", "xis1"], []])
             W(V, "ivb", "so")
             ev(V.tensor_scalar(T.mi[:], T.vb[:], T.so[:, 0:1], 1e29, A.not_equal, A.mult), "maski")
-            ev(V.tensor_scalar(T.bx2[:], T.f15[:], 32.0, None, A.mult), "bx2")
-            evs([V.quantize_mx(T.dc[:, a:a + 128], T.ds[:, a:a + 128], zeros) for a in (at(3), at(4))], "qz")
-            W(V, "maski")
-            need["maski"] = 2
-            V.tensor_scalar(T.mi[:], T.mi[:], 5e28, None, A.subtract).then_inc(T.sem.maski, 1)
+            zero("qz3", T.dc, T.ds, at(3))
             W(V, "maski", "mmi")
-            ev(V.tensor_tensor(T.mi[:], T.psi[:, 0:L], T.mi[:], A.max), "mxi")
-            ev(V.quantize_mx(T.clc[:], T.cls[:], zeros), "qcl")
-        if t == 2:
-            ev(V.tensor_copy(T.io16[:, 0:1], T.f15[:]), "io16")
+            ev(V.tensor_tensor(T.mi[:], T.psi[:, 0:L], T.mi[:], A.add), "mxi")
+            if not hub:
+                hub_constants()
+        if t == (2 if my_round == 1 else 1):
+            later_constants()
         if t > 1:
             a, b = at(t), 16 * (t - 2)
-            here = ["pc", "ps"] if t - 1 == my_round else ["ac%d" % (t - 1), "as%d" % (t - 1)]
-            W(V, here[0], "io16", "qcl")
+            W(V, "io16", "qcl")
             ev(V.tensor_copy(T.clc[:, b:b + 16].bitcast(dt.uint32), T.dc[:, a:a + 32].bitcast(dt.uint32).indirect(T.io16[:, 0:1])), "pk" + n)
-            W(S, here[1], "io16", "qcl")
+            W(S, "io16", "qcl")
             ev(S.activation(T.cls[:, b:b + 16], T.ds[:, a:a + 32].indirect(T.io16[:, 0:1]), F.Copy), "pl" + n)
-        if t == 2:
+        if t == qw_round:
             W(V, "lw")
             ev(V.quantize_mx(T.wqc[:], T.wqs[:], T.wt[:]), "qw")
-            evs([V.tensor_scalar(T[b][:], T.pi[:], k, None, A.bitwise_and) for b, k in (("p16", 16), ("p112", 112))], "ip2")
-            ev(V.tensor_scalar(T.ge0[:], T.so[:], 0.0, None, A.is_ge), "ge0")
-            W(V, "bx1", "bx2")
-            evs([V.tensor_scalar(T[b][:], T[x][:], -1.0, float(BIG - P * me), A.mult, A.add)
-                 for b, x in (("br1", "bx1"), ("br2", "bx2"))], "br")
-            W(V, "ip2")
-            ev(V.tensor_scalar(T.hh[:], T.p16[:], 0.0625, None, A.mult), "hh")
-            ev(V.tensor_copy(T.f112[:], T.p112[:]), "f112")
-            W(V, "ge0")
-            ev(V.tensor_scalar(T.val[:], T.so[:], 3.0, T.ge0[:, 0:1], A.is_le, A.mult), "val")
-            ev(V.memset(T.msg[64:128, :], 0.0), "zmsg")
-            ev(V.memset(T.pen[:], 0.0), "zpen")
-            W(V, "hh", "f112")
-            ev(V.tensor_scalar(T.hl[:], T.hh[:], -1.0, 1.0, A.mult, A.add), "hl")
-            ev(V.tensor_scalar(T.nh[:], T.hh[:], -1.0, None, A.mult), "nh")
-            ev(V.tensor_scalar(T.ch[:], T.hh[:], float(BIG - P * me), float(BIG), A.mult, A.subtract), "ch")
-            ev(V.tensor_scalar(T.g3[:], T.f112[:], 48.0, -2.0 * BIG, A.is_equal, A.mult), "g3")
-            W(V, "val", "br")
-            evs([V.tensor_scalar(T[b][:], T[x][:], T.val[:, 0:1], None, A.mult)
-                 for b, x in (("bb1", "br1"), ("bb2", "br2"))], "bb")
-        if t == 3:
-            for k in range(1, 4):
-                candidate(k)
+        if t == 2:
             numbers(1)
+        if t == 3:
             numbers(2)
-            W(V, "nv1", "nv2")
-            ev(V.tensor_tensor(T.zn[0:64, 0:2], T.nv[0:64, 0:2], T.nv[64:128, 0:2], A.max), "z12")
-            W(V, "z12")
-            ev(V.tensor_tensor(T.wn[0:32, 0:2], T.zn[0:32, 0:2], T.zn[32:64, 0:2], A.max), "w12")
-            W(V, "w12", "hl")
-            ev(V.tensor_scalar(T.en[0:32, :], T.wn[0:32, 0:1], T.hl[0:32, 0:1], float(BIG), A.mult, A.subtract), "e12")
-            W(V, "e12")
-            ev(V.tensor_scalar(T.msg[0:32, :], T.wn[0:32, 1:2], T.hh[0:32, 0:1], T.en[0:32, 0:1], A.mult, A.add), "m12")
             numbers(3)
-            W(V, "nv3")
-            ev(V.tensor_tensor(T.zn[0:64, 2:3], T.nv[0:64, 2:3], T.nv[64:128, 2:3], A.max), "z3")
-            W(V, "z3")
-            ev(V.tensor_scalar(T.wn[32:64, 2:3], T.zn[0:32, 2:3], T.zn[32:64, 2:3], T.hl[32:64, 0:1], A.max, A.mult), "w3")
-            W(V, "w3", "ch")
-            ev(V.tensor_scalar(T.e3[32:64, :], T.wn[32:64, 2:3], T.ch[32:64, 0:1], None, A.add), "e3")
 
     if my_round == R:
         cdone, sdone, ndone, nsrc = "pc", "ps", "nbo", T.nbo
@@ -454,8 +409,7 @@ def rank_program(g, core, T, topo):
     store(Y, T.y[:], T.ys[:])
     W(S, ndone)
     store(S, T.nb[:], nsrc[0:64, 0:1])
-    g.wait_ge(T.sem.loc, local[0])
     for k in sorted(need):
-        if k not in waited:
+        if k not in waited and need[k]:
             W(g, k)
     g.wait_ge(T.sem.out, outs[0])

from concourse.bass import DstId, RemoteDMATransfer
from concourse.mybir import dt, AluOpType, AxisListType, ActivationFunctionType

P, R = 512, 4
NB = 16
L = 128
H = 256
D0 = 128
KON1 = (4, 8, 8, 8)
KON2 = (8, 8, 8, 8)
ALTERNATE = False
AHEAD = (1, 2, 3)
BIG = 8192

C4, U8, F32, I32, U16, BF = "float8_e4m3fn_x4", "uint8", "float32", "int32", "uint16", "bfloat16"
_SBUF = {
    "xt": (4 * P, BF), "wt": (512, BF),
    "sd": (640, BF),
    "xqc": (P, C4), "xqs": (P, U8),
    "xic": (P, C4), "xis": (P, U8),
    "wqc": (128, C4), "wqs": (128, U8),
    "dc": (640, C4), "ds": (640, U8),
    "clc": (128, C4), "cls": (128, U8),
    "cdc": (64, C4), "cds": (64, U8),
    "cwc": (128, C4), "cws": (128, U8),
    "mk": (32, F32),
    "mn": (32, F32),
    "msg": (1, F32),
    "wmk": (16, F32),
    "nbl": (1, F32),
    "nbo": (1, F32), "m": (L, F32), "mi": (L, F32), "pm": (L * R, F32), "sg": (L, BF), "acc": (4, F32),
    "acc8": (1, F32), "pm8": (8, F32), "sg8": (8, F32), "pen": (8, F32), "vv": (8, F32),
    "offx": (8, U16), "offh": (2, U16), "io16": (2, U16), "xl": (32, U16),
    "pi": (2, I32), "p15": (2, I32), "p96": (1, I32), "p12": (1, I32), "p16": (1, I32),
    "f15": (1, F32), "so": (1, F32), "va": (L, F32), "vb": (L, F32), "vl": (32, F32), "fl": (1, F32),
    "bfd": (2, F32), "bx1": (1, F32), "bx2": (1, F32),
    "kn": (8, F32),
    "en": (4, F32), "qn": (4, F32), "an": (2, F32), "ys": (64, F32),
}
SCRATCH = {k: ("sbuf", [128, n], d) for k, (n, d) in _SBUF.items()}
SCRATCH.update({"ps": ("psum", [128, 2048], F32), "psi": ("psum", [128, 512], F32), "psy": ("psum", [128, 512], F32)})
_ROUND = ["mm", "mx", "sc", "sg", "of", "xc", "xs", "ac", "as", "wm", "qn", "en", "nv", "pk", "pl"]
SEMAPHORES = (["%s%d" % (k, t) for k in _ROUND for t in range(1, R + 1)]
              + ["lsd", "lx0", "lx1", "lx2", "lw", "zs", "sd2", "qz1", "qsd", "qz2", "qz3", "qz4", "qcl", "qx0", "qx1", "qx2", "qw",
                 "ipi", "iva", "ivb", "ivl", "ipt", "ip2", "f15", "so", "mask", "maski", "bx", "zpm", "zp8", "kn",
                 "bfd", "io16", "fl", "xl", "xic0", "xis0", "xic1", "xis1", "mmi", "mxi", "zmsg",
                 "zpen", "hm", "hc", "hs", "hn", "mkc", "s8", "sg8", "o8", "pc", "ps", "pen", "mnc",
                 "vv", "nbo", "nbl", "msg", "my", "yc", "out", "loc", "wgo"])


def rank_program(g, core, T, topo):
    me = T.rank_of(core)
    if me is None:
        return
    A, X, F = AluOpType, AxisListType.X, ActivationFunctionType
    cores = list(T.cores)
    V, S, E, Y = g.vector, g.scalar, g.tensor, g.sync

    def near(a, b):
        return cores[b] in topo.cores_of(cores[a])

    def linked(a, b):
        return topo.mates(cores[a], cores[b]) or topo.same_plane(cores[a], cores[b])

    def same_die(a, b):
        return topo.die(cores[a]) == topo.die(cores[b])

    pairs = [(a, b) for a in range(8) for b in range(a + 1, 8)
             if not near(a, b) and not linked(a, b) and not same_die(a, b)]
    if ALTERNATE:
        rest, pairs = pairs[1:], pairs[:1]
        while rest:
            nxt = [p for p in rest if not any(near(a, b) for a in p for b in pairs[-1])][0]
            rest.remove(nxt)
            pairs.append(nxt)
    my_round = [t for t in range(1, R + 1) if me in pairs[t - 1]][0]

    def engines(a, b, kon):
        if not near(a, b):
            return topo.engines(cores[a], cores[b])
        far = [c for c in range(8) if not near(a, c)][0]
        off = topo.engines(cores[a], cores[far])
        return [e for e in topo.engines(cores[a], cores[b]) if e not in off][:kon]

    def served(h, pair):
        return [d for d in range(8) if d not in pair and (near(h, d) or linked(h, d) and same_die(h, d))]

    need, waited = {}, set()

    def ev(ins, name, n=1):
        ins.then_inc(T.sem[name], n)
        need[name] = n

    def evs(calls, name):
        for ins in calls:
            ins.then_inc(T.sem[name], 1)
        need[name] = len(calls)

    def W(q, *names):
        for k in names:
            q.wait_ge(T.sem[k], need[k])
            waited.add(k)

    need["loc"] = need["wgo"] = 0

    def send(src, dst, dests, sem, kon, local="loc"):
        trs = []
        for group in ([d for d in dests if not near(me, d)], [d for d in dests if near(me, d)]):
            if not group:
                continue
            es = engines(me, group[0], kon)
            ids = []
            for d in group:
                rid, pid = topo.addr(cores[d], core)
                ids.append(DstId(rid=rid, pnc=pid))
            trs.append(RemoteDMATransfer(dst_ids=ids, dma_engine_mask=sum(1 << e for e in es), remote_sem=T.sem[sem],
                                         srcs=[src], dsts=[dst for _ in group]))
            need[local] += len(es)
        g.remote_dma_fused(trs, local_sem=T.sem[local])

    n7 = sum(len(engines(s, me, KON1[my_round - 1])) for s in range(8) if s != me)
    for k in ("hm", "hc", "hs") + (("hn",) if my_round == R else ()):
        need[k] = n7
    for t in range(1, R + 1):
        if t != my_round:
            h = [h for h in pairs[t - 1] if me in served(h, pairs[t - 1])][0]
            for k in ("ac%d" % t, "as%d" % t, "wm%d" % t if t < R else "nbl"):
                need[k] = len(engines(h, me, KON2[t - 1]))

    def quarter(q):
        return slice(32 * q, 32 * q + 32)

    lo, hi = slice(0, 64), slice(64, 128)

    def at(t):
        return D0 + 128 * (t - 1)

    parts = ((0, H), (H, H + L), (H + L, P))
    ev(Y.dma_start(T.sd[:, 0:64], T.seed[:]), "lsd", 16)
    for j, (a, b) in enumerate(parts):
        ev(Y.dma_start(T.xt[:, 4 * a:4 * b], T.x[:, 4 * a:4 * b]), "lx%d" % j, 16)

    zeros = T.sd[:, 128:640]

    def zero(name, c, s, a):
        ev(V.quantize_mx(c[:, a:a + 128], s[:, a:a + 128], zeros), name)

    ev(g.iota(T.pi[:], [[0, 2]], 0, 1), "ipi")
    ev(g.iota(T.va[:], [[1, 4], [0, 32]], 0, 0, allow_small_or_imprecise_dtypes=True), "iva")
    ev(g.iota(T.vl[:], [[128, 4], [4, 8]], 0, 0, allow_small_or_imprecise_dtypes=True), "ivl")
    ev(g.iota(T.vb[:], [[0, 32], [1, 4]], 0, 0, allow_small_or_imprecise_dtypes=True), "ivb")
    ev(V.memset(zeros, 0.0), "zs")
    W(V, "ipi")
    evs([V.tensor_scalar(T.p15[:], T.pi[:], 15, None, A.bitwise_and)]
        + [V.tensor_scalar(T[b][:], T.pi[:, 0:1], k, None, A.bitwise_and) for b, k in (("p96", 96), ("p12", 12))], "ipt")
    W(V, "zs")
    zero("qz1", T.dc, T.ds, 0)
    W(V, "ipt")
    ev(V.tensor_copy(T.f15[:], T.p15[:, 0:1]), "f15")
    evs([V.tensor_scalar(T.bx1[:], T.p12[:], 32.0, None, A.mult),
         V.tensor_scalar(T.bx2[:], T.p15[:, 0:1], 32.0, None, A.mult)], "bx")
    W(V, "f15")
    ev(V.tensor_scalar(T.so[:], T.p96[:], -0.125, T.f15[:, 0:1], A.mult, A.add), "so")
    ev(V.memset(T.pm[hi, L - 1:L * R:L], 0.0), "zpm")
    W(V, "so", "iva")
    ev(V.tensor_scalar(T.m[:], T.va[:], T.so[:, 0:1], 1e29, A.not_equal, A.mult), "mask")
    W(V, "lsd")
    ev(V.tensor_copy(T.sd[:, 64:128], T.sd[:, 0:64]), "sd2")
    W(V, "sd2")
    ev(V.quantize_mx(T.dc[:, D0:D0 + 128], T.ds[:, D0:D0 + 128], T.sd[:, 0:512]), "qsd")
    W(V, "mask", "bx")
    for j, (a, b) in enumerate(parts):
        W(V, "lx%d" % j)
        ev(V.quantize_mx(T.xqc[:, a:b], T.xqs[:, a:b], T.xt[:, 4 * a:4 * b]), "qx%d" % j)
    W(g, "zpm")

    def pm(t, a, b, s=1, rows=slice(0, 128)):
        return T.pm[rows, L * (t - 1) + a:L * (t - 1) + b:s]

    def last(t, rows=slice(0, 128)):
        return pm(t, L - 1, L, 1, rows)

    def product(bank, t, xc, xs, name, waits):
        for k in range(4):
            W(E, *waits[k])
            a = at(t) - 32 * k
            ins = E.matmul_mx(bank, T.dc[:, a:a + 128], T.ds[:, a:a + 128],
                              xc[:, L * k:L * k + L], xs[:, L * k:L * k + L], k == 0, k == 3)
        ev(ins, name)

    def hub_constants():
        ev(V.tensor_scalar(T.bfd[lo, :], T.p15[lo, :], 0.0625, None, A.mult), "bfd")
        ev(V.memset(T.pm8[hi, :], 0.0), "zp8")

    def alternate(j):
        off = T.xl[:, 16 * j:16 * j + 16]
        W(V, "xl")
        ev(V.tensor_copy(T.xic[:, H * j:H * j + H].bitcast(dt.uint32), T.xqc[:].bitcast(dt.uint32).indirect(off)), "xic%d" % j)
        W(S, "xl")
        ev(S.activation(T.xis[:, H * j:H * j + H], T.xqs[:].indirect(off), F.Copy), "xis%d" % j)

    def later_constants():
        zero("qz4", T.dc, T.ds, at(4))
        zero("qcl", T.clc, T.cls, 0)
        ev(V.tensor_copy(T.io16[:, 0:1], T.f15[:]), "io16")
        ev(V.tensor_scalar(T.p16[:], T.pi[:, 0:1], 16, None, A.bitwise_and), "ip2")
        ev(V.memset(T.msg[hi, :], 0.0), "zmsg")
        if my_round == R:
            ev(V.memset(T.pen[:], 0.0), "zpen")
        W(V, "ip2")
        k = float(BIG - P * me)
        evs([V.tensor_scalar(T.kn[lo, j:j + 1], T.p16[lo, :], a / 16, b, A.mult, A.add)
             for j, (a, b) in enumerate(((1.0, -1.0), (-1.0, 0.0), (-k, k), (k, 0.0), (k, -float(BIG)), (2.0 * BIG, 0.0)))], "kn")

    def numbers(t):
        q, h = quarter((t - 1) // 2), (t - 1) % 2
        W(V, "kn")
        ev(V.tensor_scalar(T.qn[q, t - 1:t], T.offx[q, 2 * t - 2:2 * t - 1], T.kn[q, h:h + 1], T.kn[q, 2 + h:3 + h], A.mult, A.add),
           "qn%d" % t)
        if t == my_round:
            wm = T.pm8[quarter(0), 7:8]
        else:
            W(V, "wm%d" % t)
            wm = T.wmk[quarter(0), 4 * t - 4:4 * t - 3]
        ev(V.tensor_scalar(T.en[q, t - 1:t], last(t, quarter(0)), last(t, quarter(1)), wm, A.min, A.is_equal), "en%d" % t)
        W(V, "qn%d" % t, "en%d" % t)
        if t == 1:
            ins = V.tensor_scalar(T.an[q, 0:1], T.en[q, 0:1], T.qn[q, 0:1], float(BIG), A.mult, A.subtract)
        elif t == 2:
            W(V, "nv1")
            ins = V.tensor_scalar(T.msg[q, :], T.en[q, 1:2], T.qn[q, 1:2], T.an[q, 0:1], A.mult, A.add)
        else:
            ins = V.tensor_scalar(T.an[q, 1:2], T.en[q, 2:3], T.qn[q, 2:3], T.kn[q, 4:5], A.mult, A.add)
        ev(ins, "nv%d" % t)

    w_round = 2 if my_round == 1 else 1
    qw_round = 3 if my_round <= 2 else 2

    for t in range(1, R + 1):
        pair, hub = pairs[t - 1], t == my_round
        n = str(t)
        k1, k2 = KON1[t - 1], KON2[t - 1]
        bank = T.ps[:, 512 * (t - 1):512 * (t - 1) + L]
        if t == 1:
            product(bank, 1, T.xqc, T.xqs, "mm1", [["qz1", "qsd", "qx0"], [], ["qx1"], ["qx2"]])
        else:
            here = ["pc", "ps"] if t - 1 == my_round else ["ac%d" % (t - 1), "as%d" % (t - 1)]
            product(bank, t, T.xic, T.xis, "mm" + n, [["qz" + n] + here, [], [], []])
        marks = T.m if t == 1 else T.mi
        if t == 2:
            W(V, "mxi")
        if t > 1:
            W(V, "qz%d" % (t + 1) if t < R else "qcl")
        W(V, "mm" + n)
        ev(V.tensor_tensor(marks[:], bank, marks[:], A.add if t == 1 else A.max), "mx" + n)
        W(V, "mx" + n)
        ev(V.tensor_tensor_scan(pm(t, 0, L, 1, lo), marks[lo, :], marks[hi, :], 9e29, A.min, A.min), "sc" + n)
        W(S, "sc" + n)
        if t == 1:
            ev(S.activation(T.sg[lo, :], pm(t, 0, L, 1, lo), F.Sign, bias=last(t, lo), scale=-1.0,
                            accum_out=T.acc[lo, 0:1]), "sg1")
            W(V, "sc1")
            zero("qz2", T.dc, T.ds, at(2))
        else:
            ev(S.activation(T.sg[lo, 0:32], pm(t, 3, L, 4, lo), F.Sign, bias=last(t, lo), scale=-1.0,
                            accum_out=T.acc[lo, t - 1:t]), "sg" + n)
        hubs = [h for h in pair if h != me]
        W(g, "sc" + n)
        send(last(t), T.mk[:, 4 * me:4 * me + 1], hubs, "hm", k1)
        W(V, "sg" + n)
        bx = T.bx1 if t == 1 else T.bx2
        o = 2 * (t - 1)
        evs([V.tensor_scalar(T.offx[quarter(q), o:o + 1], bx[quarter(q), 0:1], T.acc[quarter(0), t - 1:t],
                             T.acc[quarter(1), t - 1:t], A.subtract, A.subtract) for q in range(4)], "of" + n)
        offx = T.offx[:, o:o + 1]
        if hub:
            cc, cs = T.cwc[:, NB * me:NB * me + NB], T.cws[:, NB * me:NB * me + NB]
        else:
            cc, cs = T.cdc[:, NB * (t - 1):NB * t], T.cds[:, NB * (t - 1):NB * t]
        if t == 1:
            W(V, "qz2")
        W(V, "of" + n)
        ev(V.tensor_copy(cc.bitcast(dt.uint32), T.xqc[:, 0:P].bitcast(dt.uint32).indirect(offx)), "xc" + n)
        W(S, "of" + n)
        ev(S.activation(cs, T.xqs[:, 0:P].indirect(offx), F.Copy), "xs" + n)
        W(g, "xc" + n)
        send(cc.bitcast(dt.uint8), T.cwc[:, NB * me:NB * me + NB].bitcast(dt.uint8), hubs, "hc", k1)
        W(g, "xs" + n)
        send(cs, T.cws[:, NB * me:NB * me + NB], hubs, "hs", k1, "wgo" if t == w_round else "loc")
        if t == R:
            q = quarter(1)
            W(V, "nv3", "zmsg")
            ev(V.tensor_scalar(T.msg[q, :], T.offx[q, o:o + 1], T.kn[q, 1:2], T.an[q, 1:2], A.mult, A.add), "msg")
            W(g, "msg", "nv2", "zmsg")
            send(T.msg[:], T.mn[:, 4 * me:4 * me + 1], hubs, "hn", k1)
        if t == 1:
            if hub:
                hub_constants()
            ev(V.tensor_scalar(T.fl[:], T.p12[:], -31.75, T.bx2[:, 0:1], A.mult, A.add), "fl")
        if hub:
            ev(V.tensor_copy(T.mk[lo, 4 * me:4 * me + 1], last(t, lo)), "mkc")
        if t == 1:
            W(V, "fl", "ivl")
            ev(V.tensor_scalar(T.xl[:], T.vl[:], T.fl[:, 0:1], None, A.add), "xl")
            alternate(0)

        if hub:
            if t == R:
                W(V, "msg", "nv2", "zmsg")
                ev(V.tensor_copy(T.mn[:, 4 * me:4 * me + 1], T.msg[:]), "mnc")
            W(V, "mkc", "bfd", "xc" + n, "hm")
            evs([V.tensor_tensor_scan(T.pm8[quarter(q), :], T.mk[quarter(0), 0:32:4], T.mk[quarter(1), 0:32:4], 9e29, A.min, A.min)
                 for q in range(2)], "s8")
            W(S, "qz%d" % (t + 1) if t < R else "qcl", "xs" + n, "s8")
            ev(S.activation(T.sg8[lo, :], T.pm8[lo, :], F.Sign, bias=T.pm8[lo, 7:8], scale=-1.0, accum_out=T.acc8[lo, :]), "sg8")
            dests = served(me, pair)
            if t < R:
                W(g, "zp8")
            if t in AHEAD:
                W(g, "s8")
                send(T.pm8[:, 7:8], T.wmk[:, 4 * t - 4:4 * t - 3], dests, "wm" + n, k2)
            W(V, "sg8")
            evs([V.tensor_scalar(T.offh[half, :], T.bfd[lo, :], T.acc8[lo, 0:1], 16.0, A.subtract, A.mult)
                 for half in (lo, hi)], "o8")
            if t < R:
                a, k = at(t + 1), 2
                wc, ws = T.dc[:, a:a + 32], T.ds[:, a:a + 32]
            else:
                k = 1
                wc, ws = T.clc[:, 48:64], T.cls[:, 48:64]
                W(S, "sg8", "kn", "zpen")
                ev(S.activation(T.pen[quarter(1), :], T.sg8[quarter(1), :], F.Identity, scale=T.kn[quarter(1), 5:6]), "pen")
            W(V, "o8", "hc")
            ev(V.tensor_copy(wc.bitcast(dt.uint32), T.cwc[:].bitcast(dt.uint32).indirect(T.offh[:, 0:k])), "pc")
            W(S, "o8", "hs")
            ev(S.activation(ws, T.cws[:].indirect(T.offh[:, 0:k]), F.Copy), "ps")
            W(g, "pc")
            send(wc.bitcast(dt.uint8), wc.bitcast(dt.uint8), dests, "ac" + n, k2)
            W(g, "ps")
            send(ws, ws, dests, "as" + n, k2)
            if t < R and t not in AHEAD:
                send(T.pm8[:, 7:8], T.wmk[:, 4 * t - 4:4 * t - 3], dests, "wm" + n, k2)
            if t == R:
                W(V, "pen", "mnc", "hn")
                ev(V.tensor_tensor(T.vv[:], T.mn[:, 0:32:4], T.pen[:], A.add), "vv")
                W(V, "vv")
                ev(V.tensor_reduce(T.nbo[:], T.vv[:], X, A.max, negate=True), "nbo")
                W(g, "nbo")
                send(T.nbo[:], T.nbl[:], dests, "nbl", k2)

        if t == w_round:
            W(Y, "wgo")
            ev(Y.dma_start(T.wt[:], T.w[:]), "lw", 16)
        if t == 1:
            alternate(1)
            product(T.psi[:, 0:L], 1, T.xic, T.xis, "mmi", [["xic0", "xis0"], [], ["xic1", "xis1"], []])
            W(V, "ivb", "so")
            ev(V.tensor_scalar(T.mi[:], T.vb[:], T.so[:, 0:1], 1e29, A.not_equal, A.mult), "maski")
            zero("qz3", T.dc, T.ds, at(3))
            W(V, "maski", "mmi")
            ev(V.tensor_tensor(T.mi[:], T.psi[:, 0:L], T.mi[:], A.add), "mxi")
            if not hub:
                hub_constants()
        if t == (2 if my_round == 1 else 1):
            later_constants()
        if t > 1:
            a, b = at(t), 16 * (t - 2)
            W(V, "io16", "qcl")
            ev(V.tensor_copy(T.clc[:, b:b + 16].bitcast(dt.uint32), T.dc[:, a:a + 32].bitcast(dt.uint32).indirect(T.io16[:, 0:1])), "pk" + n)
            W(S, "io16", "qcl")
            ev(S.activation(T.cls[:, b:b + 16], T.ds[:, a:a + 32].indirect(T.io16[:, 0:1]), F.Copy), "pl" + n)
        if t == qw_round:
            W(V, "lw")
            ev(V.quantize_mx(T.wqc[:], T.wqs[:], T.wt[:]), "qw")
        if t == 2:
            numbers(1)
        if t == 3:
            numbers(2)
            numbers(3)

    if my_round == R:
        cdone, sdone, ndone, nsrc = "pc", "ps", "nbo", T.nbo
    else:
        cdone, sdone, ndone, nsrc = "ac4", "as4", "nbl", T.nbl
    pk, pl = ["pk2", "pk3", "pk4"], ["pl2", "pl3", "pl4"]
    W(E, "qw", "qcl", *pk)
    W(E, *pl)
    W(E, cdone, sdone)
    ev(E.matmul_mx(T.psy[:, 0:128], T.wqc[:], T.wqs[:], T.clc[:], T.cls[:], True, True), "my")
    W(V, "my")
    ev(V.tensor_copy(T.ys[:], T.psy[:, 0:64]), "yc")
    outs = [0]

    def store(q, a, b):
        q.dma_start(a, b).then_inc(T.sem.out, 16)
        outs[0] += 16

    W(Y, *pk)
    W(Y, cdone)
    store(Y, T.oc[:], T.clc[:, 0:64].bitcast(dt.uint8))
    W(Y, *pl)
    W(Y, sdone)
    store(Y, T.osc[0:4, :], T.cls[0:4, 0:64])
    W(S, *pl)
    W(S, sdone)
    for k in range(1, 4):
        store(S, T.osc[4 * k:4 * k + 4, :], T.cls[32 * k:32 * k + 4, 0:64])
    W(Y, "yc")
    store(Y, T.y[:], T.ys[:])
    W(S, ndone)
    store(S, T.nb[:], nsrc[0:64, 0:1])
    for k in sorted(need):
        if k not in waited and need[k]:
            W(g, k)
    g.wait_ge(T.sem.out, outs[0])
